import numpy as np
import ml_dtypes


def mxq(x, axis, fmt="e4m3"):
    dtype, down = {"e4m3": (ml_dtypes.float8_e4m3fn, 7), "e5m2": (ml_dtypes.float8_e5m2, 14)}[fmt]
    v = np.moveaxis(np.asarray(x, np.float32).astype(ml_dtypes.bfloat16).astype(np.float64), axis, -1)
    blocks = v.reshape(v.shape[:-1] + (-1, 32))
    amax = np.abs(blocks).max(-1, keepdims=True)
    byte = np.maximum(np.where(amax > 0, np.frexp(amax)[1] - 1 + 127, 0) - down, 1)
    scale = np.exp2(byte - 127.0)
    codes = (blocks / scale).astype(np.float32).astype(dtype).astype(np.float64)
    return np.moveaxis((codes * scale).reshape(v.shape), -1, axis)


WIDE = False


def mx_kscale(k):
    if not WIDE:
        return np.ones(k)
    levels = np.array([10, -10, 5, -5, 0])
    if k % 512:
        return np.exp2(np.random.permutation(np.resize(levels, k // 32))).repeat(32)
    a = np.empty((k // 512, 16))
    for p in range(k // 512):
        a[p, :8] = np.random.permutation(np.resize(levels, 8))
        for g in range(8):
            far = levels[np.abs(levels - a[p, g]) >= 10]
            a[p, g + 8] = far[np.random.randint(len(far))]
    return np.exp2(a.ravel()).repeat(32)


def f64(x):
    return np.asarray(x).astype(np.float64)


def striped(idx):
    return np.tile(idx.reshape(-1, 16).T, (8, 1)).astype(np.uint16)


def unstriped(offs):
    return offs[:16].T.reshape(-1).astype(np.int64)


def pack_weight(w):
    k, n = w.shape
    w = f64(np.asarray(w, np.float32).astype(ml_dtypes.bfloat16)).reshape(k // 32, 32, n)
    amax = np.abs(w).max(1)
    byte = np.clip(np.where(amax > 0, np.frexp(amax)[1] - 1 + 127 - 7, 1), 1, 254)
    scaled = (w * np.exp2(127.0 - byte)[:, None, :]).reshape(k, n).astype(np.float32)
    words = np.ascontiguousarray(scaled.reshape(k // 512, 128, 4, n).transpose(0, 1, 3, 2)).astype(ml_dtypes.float8_e4m3fn).view(np.uint8)
    return words, np.ascontiguousarray(byte.astype(np.uint8).reshape(k // 512, 16, n))


def unpack_weight(words, scales):
    g, p, n, _ = words.shape
    vals = np.ascontiguousarray(words).view(ml_dtypes.float8_e4m3fn).astype(np.float64) * np.repeat(np.exp2(scales.astype(np.float64) - 127.0), 8, axis=1)[..., None]
    return vals.transpose(0, 1, 3, 2).reshape(g * 512, n)

def planes(y):
    n, m = y.shape
    v = y.astype(np.float32).astype(ml_dtypes.bfloat16).astype(np.float64).reshape(n // 32, 32, m)
    top = np.abs(v).max(1)
    byte = np.clip(np.where(top > 0, np.frexp(top)[1] - 1 + 127 - 7, 1), 1, 254)
    codes = (v * np.exp2(127.0 - byte)[:, None, :]).reshape(n, m).astype(np.float32).astype(ml_dtypes.float8_e4m3fn).view(np.uint8)
    words = codes.reshape(n // 512, 128, 4, m).transpose(0, 1, 3, 2)
    return np.ascontiguousarray(words), np.ascontiguousarray(byte.astype(np.uint8).reshape(n // 512, 16, m))


K, T, S, N = 512, 1024, 512, 512
P = 2 ** 7


def setup_inputs():
    n = np.random.standard_normal
    s = mx_kscale(K)[:, None]
    packed_xT = pack_weight(n((K, T)) * s)
    return {
        "x_words": packed_xT[0],
        "x_scales": packed_xT[1],
        "gate": np.tile(np.random.uniform(0.2, 1.0, T), (P, 1)).astype(np.float32),
        "w1": (n((K, N)) / np.sqrt(K) / s).astype(np.float32),
        "offs": striped(np.random.permutation(T)[:S]),
    }


def reference(x_words, x_scales, gate, w1, offs):
    xq = unpack_weight(x_words, x_scales)[:, unstriped(offs)]
    y = mxq(f64(w1), 0, "e4m3").T @ xq
    g = f64(gate)[:1][:, unstriped(offs)]
    out = np.zeros((N, T))
    out[:, unstriped(offs)] = y * g
    return (out,) + planes(out)

@@ -1,0 +1,136 @@
+from contextlib import ExitStack
+
+import concourse.mybir as mybir
+
+K, T, S, N = 512, 1024, 512, 512
+FLOPS = 2 * K * S * N
+
+F32 = mybir.dt.float32
+BF16 = mybir.dt.bfloat16
+I32 = mybir.dt.int32
+U32 = mybir.dt.uint32
+U16 = mybir.dt.uint16
+U8 = mybir.dt.uint8
+FP8X4 = mybir.dt.float8_e4m3fn_x4
+MULT = mybir.AluOpType.mult
+
+P = 128
+PACK = 4
+
+
+def tile_picked_modgate_linnone_po_kernel(
+    tc, x_words, x_scales, gate, w1, offs, out_0, out_1, out_2
+):
+    nc = tc.nc
+    with ExitStack() as ctx:
+        keep = ctx.enter_context(tc.tile_pool(name="keep", bufs=1))
+        psum = ctx.enter_context(tc.psum_pool(name="psum", bufs=1))
+
+        offsets = keep.tile([P, S // 16], U16, name="offsets")
+        nc.sync.dma_start(offsets[:], offs)
+
+        token_scales = keep.tile([P, T], U8, name="token_scales", align_bytes=64)
+        nc.vector.memset(token_scales[:].bitcast(I32), 0)
+        token_words = keep.tile([P, T], I32, name="token_words", align_bytes=64)
+        nc.sync.dma_start(token_words[:], x_words[0].rearrange("p c r -> p (c r)").bitcast(I32))
+        for q in range(4):
+            nc.sync.dma_start(
+                token_scales[32 * q : 32 * q + 4, :].bitcast(I32),
+                x_scales[0, 4 * q : 4 * q + 4, :].bitcast(I32),
+            )
+        w_rows = w1.rearrange("(p j) c -> p j c", j=PACK)
+        half = N // 2
+        w_raw = []
+        for h in range(2):
+            raw = keep.tile([P, PACK, half], F32, name=f"w_raw{h}", align_bytes=64)
+            nc.sync.dma_start(raw[:], w_rows[:, :, h * half : (h + 1) * half])
+            w_raw.append(raw)
+        scores = keep.tile([P, T], F32, name="scores", align_bytes=64)
+        nc.sync.dma_start(scores[:], gate)
+
+        placed = []
+        for t in range(PACK):
+            window = keep.tile([P, T], F32, name=f"placed{t}", align_bytes=64)
+            nc.vector.memset(window[:], 0.0)
+            placed.append(window)
+
+        picked_words = keep.tile([P, S], U32, name="picked_words", align_bytes=64)
+        nc.vector.tensor_copy(picked_words[:], token_words[:].bitcast(U32).indirect(offsets[:]))
+        picked_scales = keep.tile([P, S], U8, name="picked_scales", align_bytes=64)
+        nc.vector.tensor_copy(picked_scales[:], token_scales[:].indirect(offsets[:]))
+
+        w_bf16 = keep.tile([P, PACK, P, PACK], BF16, name="w_bf16", align_bytes=64)
+
+        def deal(engine_copy, h, m0, m1):
+            src = w_raw[h][:].rearrange("p j (m t) -> p m j t", t=PACK)[:, m0:m1]
+            dst = w_bf16[:].rearrange("p t m j -> p m j t")[:, 64 * h + m0 : 64 * h + m1]
+            engine_copy(dst, src)
+
+        deal(nc.scalar.copy, 0, 0, 64)
+        deal(nc.scalar.copy, 1, 0, 24)
+        deal(nc.vector.tensor_copy, 1, 24, 64)
+
+        results = []
+        for t in range(PACK):
+            w_codes = keep.tile([P, P], U32, name=f"w_codes{t}", align_bytes=64)
+            w_scales = keep.tile([P, P], U8, name=f"w_scales{t}", align_bytes=64)
+            nc.vector.quantize_mx(
+                out=w_codes[:].bitcast(FP8X4),
+                scales=w_scales[:],
+                in_=w_bf16[:, t].rearrange("p m j -> p (m j)"),
+            )
+            acc = psum.tile([P, S], F32, name=f"acc{t}")
+            nc.tensor.matmul_mx(
+                out=acc[:],
+                lhsT=w_codes[:].bitcast(FP8X4),
+                lhsT_scale=w_scales[:],
+                rhs=picked_words[:].bitcast(FP8X4),
+                rhs_scale=picked_scales[:],
+                start=True,
+                stop=True,
+            )
+            result = keep.tile([P, S], F32, name=f"result{t}", align_bytes=64)
+            nc.scalar.copy(result[:], acc[:])
+            results.append(result)
+
+        picked_scores = keep.tile([P, S], F32, name="picked_scores", align_bytes=64)
+        nc.vector.tensor_copy(picked_scores[:], scores[:].indirect(offsets[:]))
+
+        spans = [(0, 512), (512, 768), (768, 1024)]
+        rounded = [
+            keep.tile([P, c1 - c0, PACK], BF16, name=f"rounded{c0}", align_bytes=64) for c0, c1 in spans
+        ]
+        out_rows = out_0.rearrange("(p t) c -> t p c", t=PACK)
+        for t in range(PACK):
+            nc.vector.tensor_tensor(placed[t][:].indirect(offsets[:]), results[t][:], picked_scores[:], MULT)
+            nc.sync.dma_start(out_rows[t], placed[t][:])
+            for i, (c0, c1) in enumerate(spans):
+                if t == PACK - 1 and i == 0:
+                    nc.vector.tensor_copy(rounded[i][:, 0:256, t], placed[t][:, 0:256])
+                    nc.vector.tensor_copy(rounded[i][:, 256:512, t], placed[t][:, 256:512])
+                elif t == PACK - 2 and i == 0:
+                    both = placed[t][:, c0:c1].unsqueeze(2).to_broadcast([P, c1 - c0, 2])
+                    nc.scalar.copy(rounded[i][:, :, t : t + 2], both)
+                else:
+                    nc.scalar.copy(rounded[i][:, :, t], placed[t][:, c0:c1])
+
+        out_codes = [keep.tile([P, 512], I32, name=f"out_codes{h}", align_bytes=64) for h in range(2)]
+        out_scales = keep.tile([P, T], U8, name="out_scales", align_bytes=64)
+        words_hbm = out_1[0].rearrange("p c r -> p (c r)").bitcast(I32)
+        for c0 in range(0, T, 256):
+            i = max(0, c0 // 256 - 1)
+            lo = c0 - spans[i][0]
+            nc.vector.quantize_mx(
+                out=out_codes[c0 // 512][:, c0 % 512 : c0 % 512 + 256].bitcast(FP8X4),
+                scales=out_scales[:, c0 : c0 + 256],
+                in_=rounded[i][:, lo : lo + 256, :].rearrange("p c t -> p (c t)"),
+            )
+            if c0 % 512 == 256:
+                h = c0 // 512
+                nc.sync.dma_start(words_hbm[:, 512 * h : 512 * h + 512], out_codes[h][:])
+        for q in range(4):
+            queue = nc.scalar if q % 2 == 0 else nc.sync
+            queue.dma_start(
+                out_2[0, 4 * q : 4 * q + 4, :].bitcast(I32),
+                out_scales[32 * q : 32 * q + 4, :].bitcast(I32),
+            )

@@ -34,7 +34,7 @@ def tile_picked_modgate_linnone_po_kernel(
         token_words = keep.tile([P, T], I32, name="token_words", align_bytes=64)
         nc.sync.dma_start(token_words[:], x_words[0].rearrange("p c r -> p (c r)").bitcast(I32))
         for q in range(4):
-            nc.sync.dma_start(
+            nc.scalar.dma_start(
                 token_scales[32 * q : 32 * q + 4, :].bitcast(I32),
                 x_scales[0, 4 * q : 4 * q + 4, :].bitcast(I32),
             )
@@ -49,17 +49,18 @@ def tile_picked_modgate_linnone_po_kernel(
         nc.sync.dma_start(scores[:], gate)
 
         placed = []
-        for t in range(PACK):
+        for t in range(PACK - 1):
             window = keep.tile([P, T], F32, name=f"placed{t}", align_bytes=64)
-            nc.vector.memset(window[:], 0.0)
+            nc.vector.memset(window[:].bitcast(I32), 0)
             placed.append(window)
+        placed.append(placed[0])
 
         picked_words = keep.tile([P, S], U32, name="picked_words", align_bytes=64)
         nc.vector.tensor_copy(picked_words[:], token_words[:].bitcast(U32).indirect(offsets[:]))
         picked_scales = keep.tile([P, S], U8, name="picked_scales", align_bytes=64)
         nc.vector.tensor_copy(picked_scales[:], token_scales[:].indirect(offsets[:]))
 
-        w_bf16 = keep.tile([P, PACK, P, PACK], BF16, name="w_bf16", align_bytes=64)
+        w_bf16 = keep.tile([P, PACK, P, PACK], BF16, name="w_bf16", tag="staged", align_bytes=64)
 
         def deal(engine_copy, h, m0, m1):
             src = w_raw[h][:].rearrange("p j (m t) -> p m j t", t=PACK)[:, m0:m1]
@@ -93,41 +94,39 @@ def tile_picked_modgate_linnone_po_kernel(
             nc.scalar.copy(result[:], acc[:])
             results.append(result)
 
-        picked_scores = keep.tile([P, S], F32, name="picked_scores", align_bytes=64)
+        picked_scores = keep.tile([P, S], F32, name="picked_scores", tag="staged", align_bytes=64)
         nc.vector.tensor_copy(picked_scores[:], scores[:].indirect(offsets[:]))
 
-        spans = [(0, 512), (512, 768), (768, 1024)]
-        rounded = [
-            keep.tile([P, c1 - c0, PACK], BF16, name=f"rounded{c0}", align_bytes=64) for c0, c1 in spans
-        ]
+        rounded = keep.tile([P, T * PACK], BF16, name="rounded", align_bytes=64)
+        planes = rounded[:].rearrange("p (c t) -> p c t", t=PACK)
+        split = 640
         out_rows = out_0.rearrange("(p t) c -> t p c", t=PACK)
         for t in range(PACK):
             nc.vector.tensor_tensor(placed[t][:].indirect(offsets[:]), results[t][:], picked_scores[:], MULT)
             nc.sync.dma_start(out_rows[t], placed[t][:])
-            for i, (c0, c1) in enumerate(spans):
-                if t == PACK - 1 and i == 0:
-                    nc.vector.tensor_copy(rounded[i][:, 0:256, t], placed[t][:, 0:256])
-                    nc.vector.tensor_copy(rounded[i][:, 256:512, t], placed[t][:, 256:512])
-                elif t == PACK - 2 and i == 0:
-                    both = placed[t][:, c0:c1].unsqueeze(2).to_broadcast([P, c1 - c0, 2])
-                    nc.scalar.copy(rounded[i][:, :, t : t + 2], both)
-                else:
-                    nc.scalar.copy(rounded[i][:, :, t], placed[t][:, c0:c1])
+            if t < PACK - 2:
+                nc.scalar.copy(planes[:, :, t], placed[t][:])
+            elif t == PACK - 2:
+                both = placed[t][:, :split].unsqueeze(2).to_broadcast([P, split, 2])
+                nc.scalar.copy(planes[:, :split, t : t + 2], both)
+                nc.scalar.copy(planes[:, split:, t], placed[t][:, split:])
+            else:
+                for c0, c1 in ((0, 256), (256, split)):
+                    nc.vector.tensor_copy(planes[:, c0:c1, t], placed[t][:, c0:c1])
+                for c0, c1 in ((split, 768), (768, T)):
+                    nc.scalar.copy(planes[:, c0:c1, t], placed[t][:, c0:c1])
 
-        out_codes = [keep.tile([P, 512], I32, name=f"out_codes{h}", align_bytes=64) for h in range(2)]
         out_scales = keep.tile([P, T], U8, name="out_scales", align_bytes=64)
         words_hbm = out_1[0].rearrange("p c r -> p (c r)").bitcast(I32)
-        for c0 in range(0, T, 256):
-            i = max(0, c0 // 256 - 1)
-            lo = c0 - spans[i][0]
-            nc.vector.quantize_mx(
-                out=out_codes[c0 // 512][:, c0 % 512 : c0 % 512 + 256].bitcast(FP8X4),
-                scales=out_scales[:, c0 : c0 + 256],
-                in_=rounded[i][:, lo : lo + 256, :].rearrange("p c t -> p (c t)"),
-            )
-            if c0 % 512 == 256:
-                h = c0 // 512
-                nc.sync.dma_start(words_hbm[:, 512 * h : 512 * h + 512], out_codes[h][:])
+        for s0, s1 in ((0, 512), (512, 768), (768, T)):
+            out_codes = keep.tile([P, s1 - s0], I32, name=f"out_codes{s0}", align_bytes=64)
+            for c0 in range(s0, s1, 256):
+                nc.vector.quantize_mx(
+                    out=out_codes[:, c0 - s0 : c0 - s0 + 256].bitcast(FP8X4),
+                    scales=out_scales[:, c0 : c0 + 256],
+                    in_=rounded[:, PACK * c0 : PACK * (c0 + 256)],
+                )
+            nc.sync.dma_start(words_hbm[:, s0:s1], out_codes[:])
         for q in range(4):
             queue = nc.scalar if q % 2 == 0 else nc.sync
             queue.dma_start(

@@ -25,84 +25,137 @@ def tile_picked_modgate_linnone_po_kernel(
     with ExitStack() as ctx:
         keep = ctx.enter_context(tc.tile_pool(name="keep", bufs=1))
         psum = ctx.enter_context(tc.psum_pool(name="psum", bufs=1))
+        shared = ctx.enter_context(tc.tile_pool(name="shared", bufs=1))
 
         offsets = keep.tile([P, S // 16], U16, name="offsets")
         nc.sync.dma_start(offsets[:], offs)
 
+        score_cols = shared.tile([P, T // P], F32, name="score_cols", align_bytes=64, offset=16 * T + S)
+        nc.sync.dma_start(score_cols[:], gate[0].rearrange("(p j) -> p j", p=P))
         token_scales = keep.tile([P, T], U8, name="token_scales", align_bytes=64)
         nc.vector.memset(token_scales[:].bitcast(I32), 0)
-        token_words = keep.tile([P, T], I32, name="token_words", align_bytes=64)
-        nc.sync.dma_start(token_words[:], x_words[0].rearrange("p c r -> p (c r)").bitcast(I32))
-        for q in range(4):
-            nc.scalar.dma_start(
-                token_scales[32 * q : 32 * q + 4, :].bitcast(I32),
-                x_scales[0, 4 * q : 4 * q + 4, :].bitcast(I32),
+        identity = shared.tile([P, P], F32, name="identity", align_bytes=64, offset=18 * T + S)
+        for r, place in enumerate((8 * T + S - 128, 4 * T)):
+            ramp = shared.tile([P, P // 2], F32, name=f"ramp{r}", align_bytes=64, offset=place)
+            nc.gpsimd.iota(
+                ramp[:], [[1, P // 2]], base=r * P // 2, channel_multiplier=-1, allow_small_or_imprecise_dtypes=True
+            )
+            nc.vector.tensor_scalar(
+                identity[:, r * P // 2 : (r + 1) * P // 2], ramp[:], 0.0, None, mybir.AluOpType.is_equal
             )
         w_rows = w1.rearrange("(p j) c -> p j c", j=PACK)
         half = N // 2
         w_raw = []
         for h in range(2):
-            raw = keep.tile([P, PACK, half], F32, name=f"w_raw{h}", align_bytes=64)
+            raw = shared.tile([P, PACK, half], F32, name=f"w_raw{h}", align_bytes=64, offset=(12 - 4 * h) * T + S)
             nc.sync.dma_start(raw[:], w_rows[:, :, h * half : (h + 1) * half])
             w_raw.append(raw)
-        scores = keep.tile([P, T], F32, name="scores", align_bytes=64)
-        nc.sync.dma_start(scores[:], gate)
+            if h == 0:
+                for q in range(4):
+                    nc.sync.dma_start(
+                        token_scales[32 * q : 32 * q + 4, :].bitcast(I32),
+                        x_scales[0, 4 * q : 4 * q + 4, :].bitcast(I32),
+                    )
+        token_words = shared.tile([P, T], I32, name="token_words", align_bytes=64, offset=4 * T + S)
+        nc.sync.dma_start(token_words[:], x_words[0].rearrange("p c r -> p (c r)").bitcast(I32))
 
         placed = []
         for t in range(PACK - 1):
             window = keep.tile([P, T], F32, name=f"placed{t}", align_bytes=64)
-            nc.vector.memset(window[:].bitcast(I32), 0)
+            nc.gpsimd.memset(window[:], 0.0)
             placed.append(window)
         placed.append(placed[0])
 
-        picked_words = keep.tile([P, S], U32, name="picked_words", align_bytes=64)
-        nc.vector.tensor_copy(picked_words[:], token_words[:].bitcast(U32).indirect(offsets[:]))
-        picked_scales = keep.tile([P, S], U8, name="picked_scales", align_bytes=64)
+        scores = shared.tile([P, T], F32, name="scores", align_bytes=64, offset=0)
+        for b in range(2):
+            spread = psum.tile([P, PACK, P], F32, name=f"spread{b}")
+            for j in range(PACK):
+                col = PACK * b + j
+                nc.tensor.transpose(
+                    spread[:, j, :], score_cols[:, col : col + 1].to_broadcast([P, P]), identity[:]
+                )
+            nc.scalar.copy(
+                scores[:].rearrange("p (n j) -> p n j", j=T // P)[:, :, PACK * b : PACK * (b + 1)],
+                spread[:].rearrange("p j n -> p n j"),
+            )
+
+        HS = S // 2
+        w_bf16 = [
+            shared.tile([P, 2, P, PACK], BF16, name=f"w_bf16_{u}", align_bytes=64, offset=(16 + 2 * u) * T + S)
+            for u in range(2)
+        ]
+
+        def deal(u, h):
+            src = w_raw[h][:].rearrange("p j (m t) -> p m j t", t=PACK)[:, :, :, 2 * u : 2 * u + 2]
+            dst = w_bf16[u][:].rearrange("p t m j -> p m j t")[:, 64 * h : 64 * (h + 1)]
+            nc.scalar.copy(dst, src)
+
+        picked_scales = shared.tile([P, S], U8, name="picked_scales", align_bytes=64, offset=4 * T)
         nc.vector.tensor_copy(picked_scales[:], token_scales[:].indirect(offsets[:]))
+        deal(0, 0)
+        deal(0, 1)
+        deal(1, 0)
+        deal(1, 1)
+        picked_scores = keep.tile([P, S], F32, name="picked_scores", align_bytes=64)
+        nc.vector.tensor_copy(picked_scores[:], scores[:].indirect(offsets[:]))
+        picked_words = [
+            shared.tile([P, HS], U32, name=f"picked_words{a}", align_bytes=64, offset=16 * T + S + 4 * HS * a)
+            for a in range(2)
+        ]
 
-        w_bf16 = keep.tile([P, PACK, P, PACK], BF16, name="w_bf16", tag="staged", align_bytes=64)
-
-        def deal(engine_copy, h, m0, m1):
-            src = w_raw[h][:].rearrange("p j (m t) -> p m j t", t=PACK)[:, m0:m1]
-            dst = w_bf16[:].rearrange("p t m j -> p m j t")[:, 64 * h + m0 : 64 * h + m1]
-            engine_copy(dst, src)
-
-        deal(nc.scalar.copy, 0, 0, 64)
-        deal(nc.scalar.copy, 1, 0, 24)
-        deal(nc.vector.tensor_copy, 1, 24, 64)
-
-        results = []
-        for t in range(PACK):
-            w_codes = keep.tile([P, P], U32, name=f"w_codes{t}", align_bytes=64)
+        def quantise_weights(t):
+            if t < 2:
+                w_codes = keep.tile([P, P], U32, name=f"w_codes{t}", align_bytes=64)
+            else:
+                w_codes = shared.tile([P, P], U32, name=f"w_codes{t}", align_bytes=64, offset=4 * T + S * (t - 1))
             w_scales = keep.tile([P, P], U8, name=f"w_scales{t}", align_bytes=64)
             nc.vector.quantize_mx(
                 out=w_codes[:].bitcast(FP8X4),
                 scales=w_scales[:],
-                in_=w_bf16[:, t].rearrange("p m j -> p (m j)"),
+                in_=w_bf16[t // 2][:, t % 2].rearrange("p m j -> p (m j)"),
             )
-            acc = psum.tile([P, S], F32, name=f"acc{t}")
+            return w_codes, w_scales
+
+        def product(acc, weights, a):
             nc.tensor.matmul_mx(
-                out=acc[:],
-                lhsT=w_codes[:].bitcast(FP8X4),
-                lhsT_scale=w_scales[:],
-                rhs=picked_words[:].bitcast(FP8X4),
-                rhs_scale=picked_scales[:],
+                out=acc,
+                lhsT=weights[0][:].bitcast(FP8X4),
+                lhsT_scale=weights[1][:],
+                rhs=picked_words[a][:].bitcast(FP8X4),
+                rhs_scale=picked_scales[:, a * HS : (a + 1) * HS],
                 start=True,
                 stop=True,
             )
-            result = keep.tile([P, S], F32, name=f"result{t}", align_bytes=64)
-            nc.scalar.copy(result[:], acc[:])
-            results.append(result)
 
-        picked_scores = keep.tile([P, S], F32, name="picked_scores", tag="staged", align_bytes=64)
-        nc.vector.tensor_copy(picked_scores[:], scores[:].indirect(offsets[:]))
+        results = [keep.tile([P, S], F32, name=f"result{t}", align_bytes=64) for t in range(PACK)]
+        weights = quantise_weights(0)
+        for a in range(2):
+            nc.vector.tensor_copy(
+                picked_words[a][:],
+                token_words[:].bitcast(U32).indirect(offsets[:, a * HS // 16 : (a + 1) * HS // 16]),
+            )
+            acc = psum.tile([P, HS], F32, name=f"acc0_{a}")
+            product(acc[:], weights, a)
+            nc.scalar.copy(results[0][:, a * HS : (a + 1) * HS], acc[:])
+        for t in range(1, PACK):
+            weights = quantise_weights(t)
+            acc = psum.tile([P, S], F32, name=f"acc{t}")
+            for a in range(2):
+                product(acc[:, a * HS : (a + 1) * HS], weights, a)
+            nc.scalar.copy(results[t][:], acc[:])
 
         rounded = keep.tile([P, T * PACK], BF16, name="rounded", align_bytes=64)
         planes = rounded[:].rearrange("p (c t) -> p c t", t=PACK)
-        split = 640
+        split = 512
         out_rows = out_0.rearrange("(p t) c -> t p c", t=PACK)
         for t in range(PACK):
-            nc.vector.tensor_tensor(placed[t][:].indirect(offsets[:]), results[t][:], picked_scores[:], MULT)
+            for s0, s1 in ((0, HS), (HS, S)) if t == 0 else ((0, S),):
+                nc.vector.tensor_tensor(
+                    placed[t][:].indirect(offsets[:, s0 // 16 : s1 // 16]),
+                    results[t][:, s0:s1],
+                    picked_scores[:, s0:s1],
+                    MULT,
+                )
             nc.sync.dma_start(out_rows[t], placed[t][:])
             if t < PACK - 2:
                 nc.scalar.copy(planes[:, :, t], placed[t][:])
@@ -111,21 +164,19 @@ def tile_picked_modgate_linnone_po_kernel(
                 nc.scalar.copy(planes[:, :split, t : t + 2], both)
                 nc.scalar.copy(planes[:, split:, t], placed[t][:, split:])
             else:
-                for c0, c1 in ((0, 256), (256, split)):
-                    nc.vector.tensor_copy(planes[:, c0:c1, t], placed[t][:, c0:c1])
+                nc.vector.tensor_copy(planes[:, :split, t], placed[t][:, :split])
                 for c0, c1 in ((split, 768), (768, T)):
                     nc.scalar.copy(planes[:, c0:c1, t], placed[t][:, c0:c1])
 
         out_scales = keep.tile([P, T], U8, name="out_scales", align_bytes=64)
         words_hbm = out_1[0].rearrange("p c r -> p (c r)").bitcast(I32)
-        for s0, s1 in ((0, 512), (512, 768), (768, T)):
+        for s0, s1 in ((split, 768), (0, split), (768, T)):
             out_codes = keep.tile([P, s1 - s0], I32, name=f"out_codes{s0}", align_bytes=64)
-            for c0 in range(s0, s1, 256):
-                nc.vector.quantize_mx(
-                    out=out_codes[:, c0 - s0 : c0 - s0 + 256].bitcast(FP8X4),
-                    scales=out_scales[:, c0 : c0 + 256],
-                    in_=rounded[:, PACK * c0 : PACK * (c0 + 256)],
-                )
+            nc.vector.quantize_mx(
+                out=out_codes[:].bitcast(FP8X4),
+                scales=out_scales[:, s0:s1],
+                in_=rounded[:, PACK * s0 : PACK * s1],
+            )
             nc.sync.dma_start(words_hbm[:, s0:s1], out_codes[:])
         for q in range(4):
             queue = nc.scalar if q % 2 == 0 else nc.sync

@@ -35,14 +35,9 @@ def tile_picked_modgate_linnone_po_kernel(
         token_scales = keep.tile([P, T], U8, name="token_scales", align_bytes=64)
         nc.vector.memset(token_scales[:].bitcast(I32), 0)
         identity = shared.tile([P, P], F32, name="identity", align_bytes=64, offset=18 * T + S)
-        for r, place in enumerate((8 * T + S - 128, 4 * T)):
-            ramp = shared.tile([P, P // 2], F32, name=f"ramp{r}", align_bytes=64, offset=place)
-            nc.gpsimd.iota(
-                ramp[:], [[1, P // 2]], base=r * P // 2, channel_multiplier=-1, allow_small_or_imprecise_dtypes=True
-            )
-            nc.vector.tensor_scalar(
-                identity[:, r * P // 2 : (r + 1) * P // 2], ramp[:], 0.0, None, mybir.AluOpType.is_equal
-            )
+        ramp = shared.tile([P, P], F32, name="ramp", align_bytes=64, offset=8 * T + S - 256)
+        nc.gpsimd.iota(ramp[:], [[1, P]], base=0, channel_multiplier=-1, allow_small_or_imprecise_dtypes=True)
+        nc.gpsimd.tensor_scalar(identity[:], ramp[:], 0.0, 1.0, mybir.AluOpType.is_equal, MULT)
         w_rows = w1.rearrange("(p j) c -> p j c", j=PACK)
         half = N // 2
         w_raw = []
@@ -62,7 +57,7 @@ def tile_picked_modgate_linnone_po_kernel(
         placed = []
         for t in range(PACK - 1):
             window = keep.tile([P, T], F32, name=f"placed{t}", align_bytes=64)
-            nc.gpsimd.memset(window[:], 0.0)
+            nc.vector.memset(window[:].bitcast(I32), 0)
             placed.append(window)
         placed.append(placed[0])
 

@@ -16,6 +16,15 @@ MULT = mybir.AluOpType.mult
 
 P = 128
 PACK = 4
+CUT = 192
+REST = N - CUT
+AT_SCALES = 4 * T
+AT_WORDS = AT_SCALES + S
+AT_REST = AT_WORDS + 4 * T
+AT_PLACED = AT_REST + 4 * PACK * (N - CUT)
+AT_DEALT = AT_PLACED + 4 * T * (PACK - 1)
+AT_LEAD = AT_DEALT + 4 * T
+LEAD = 128
 
 
 def tile_picked_modgate_linnone_po_kernel(
@@ -27,36 +36,38 @@ def tile_picked_modgate_linnone_po_kernel(
         psum = ctx.enter_context(tc.psum_pool(name="psum", bufs=1))
         shared = ctx.enter_context(tc.tile_pool(name="shared", bufs=1))
 
+        score_cols = shared.tile([P, T // P], F32, name="score_cols", align_bytes=64, offset=AT_DEALT)
+        nc.sync.dma_start(score_cols[:], gate[0].rearrange("(p j) -> p j", p=P))
         offsets = keep.tile([P, S // 16], U16, name="offsets")
         nc.sync.dma_start(offsets[:], offs)
 
-        score_cols = shared.tile([P, T // P], F32, name="score_cols", align_bytes=64, offset=16 * T + S)
-        nc.sync.dma_start(score_cols[:], gate[0].rearrange("(p j) -> p j", p=P))
         token_scales = keep.tile([P, T], U8, name="token_scales", align_bytes=64)
         nc.vector.memset(token_scales[:].bitcast(I32), 0)
-        identity = shared.tile([P, P], F32, name="identity", align_bytes=64, offset=18 * T + S)
-        ramp = shared.tile([P, P], F32, name="ramp", align_bytes=64, offset=8 * T + S - 256)
-        nc.gpsimd.iota(ramp[:], [[1, P]], base=0, channel_multiplier=-1, allow_small_or_imprecise_dtypes=True)
-        nc.gpsimd.tensor_scalar(identity[:], ramp[:], 0.0, 1.0, mybir.AluOpType.is_equal, MULT)
+        identity = shared.tile([P, P], F32, name="identity", align_bytes=64, offset=AT_DEALT + 2 * T)
+        ramp = shared.tile([P, (AT_DEALT - AT_SCALES) // 4], F32, name="ramp", align_bytes=64, offset=AT_SCALES)
+        nc.gpsimd.iota(ramp[:, :P], [[1, P]], base=0, channel_multiplier=-1, allow_small_or_imprecise_dtypes=True)
+        nc.vector.tensor_scalar(identity[:], ramp[:, :P], 0.0, None, mybir.AluOpType.is_equal)
         w_rows = w1.rearrange("(p j) c -> p j c", j=PACK)
-        half = N // 2
-        w_raw = []
-        for h in range(2):
-            raw = shared.tile([P, PACK, half], F32, name=f"w_raw{h}", align_bytes=64, offset=(12 - 4 * h) * T + S)
-            nc.sync.dma_start(raw[:], w_rows[:, :, h * half : (h + 1) * half])
-            w_raw.append(raw)
-            if h == 0:
-                for q in range(4):
-                    nc.sync.dma_start(
-                        token_scales[32 * q : 32 * q + 4, :].bitcast(I32),
-                        x_scales[0, 4 * q : 4 * q + 4, :].bitcast(I32),
-                    )
-        token_words = shared.tile([P, T], I32, name="token_words", align_bytes=64, offset=4 * T + S)
+        w_first = keep.tile([P, PACK, CUT], F32, name="w_first", align_bytes=64)
+        nc.sync.dma_start(w_first[:], w_rows[:, :, :CUT])
+        for q in range(4):
+            nc.sync.dma_start(
+                token_scales[32 * q : 32 * q + 4, :].bitcast(I32),
+                x_scales[0, 4 * q : 4 * q + 4, :].bitcast(I32),
+            )
+        w_raw = [(w_first, 0, CUT // PACK)]
+        for c0 in (CUT,):
+            raw = shared.tile(
+                [P, PACK, REST], F32, name=f"w_rest{c0}", align_bytes=64, offset=AT_REST + 4 * PACK * (c0 - CUT)
+            )
+            nc.sync.dma_start(raw[:], w_rows[:, :, c0 : c0 + REST])
+            w_raw.append((raw, c0 // PACK, (c0 + REST) // PACK))
+        token_words = shared.tile([P, T], I32, name="token_words", align_bytes=64, offset=AT_WORDS)
         nc.sync.dma_start(token_words[:], x_words[0].rearrange("p c r -> p (c r)").bitcast(I32))
 
         placed = []
         for t in range(PACK - 1):
-            window = keep.tile([P, T], F32, name=f"placed{t}", align_bytes=64)
+            window = shared.tile([P, T], F32, name=f"placed{t}", align_bytes=64, offset=AT_PLACED + 4 * T * t)
             nc.vector.memset(window[:].bitcast(I32), 0)
             placed.append(window)
         placed.append(placed[0])
@@ -74,83 +85,86 @@ def tile_picked_modgate_linnone_po_kernel(
                 spread[:].rearrange("p j n -> p n j"),
             )
 
-        HS = S // 2
         w_bf16 = [
-            shared.tile([P, 2, P, PACK], BF16, name=f"w_bf16_{u}", align_bytes=64, offset=(16 + 2 * u) * T + S)
+            shared.tile([P, 2, P, PACK], BF16, name=f"w_bf16_{u}", align_bytes=64, offset=AT_DEALT + 2 * u * T)
             for u in range(2)
         ]
 
         def deal(u, h):
-            src = w_raw[h][:].rearrange("p j (m t) -> p m j t", t=PACK)[:, :, :, 2 * u : 2 * u + 2]
-            dst = w_bf16[u][:].rearrange("p t m j -> p m j t")[:, 64 * h : 64 * (h + 1)]
+            raw, m0, m1 = w_raw[h]
+            src = raw[:].rearrange("p j (m t) -> p m j t", t=PACK)[:, :, :, 2 * u : 2 * u + 2]
+            dst = w_bf16[u][:].rearrange("p t m j -> p m j t")[:, m0:m1]
             nc.scalar.copy(dst, src)
 
-        picked_scales = shared.tile([P, S], U8, name="picked_scales", align_bytes=64, offset=4 * T)
+        picked_scales = shared.tile([P, S], U8, name="picked_scales", align_bytes=64, offset=AT_SCALES)
         nc.vector.tensor_copy(picked_scales[:], token_scales[:].indirect(offsets[:]))
-        deal(0, 0)
-        deal(0, 1)
-        deal(1, 0)
-        deal(1, 1)
+        for u in range(2):
+            for h in range(2):
+                deal(u, h)
         picked_scores = keep.tile([P, S], F32, name="picked_scores", align_bytes=64)
         nc.vector.tensor_copy(picked_scores[:], scores[:].indirect(offsets[:]))
-        picked_words = [
-            shared.tile([P, HS], U32, name=f"picked_words{a}", align_bytes=64, offset=16 * T + S + 4 * HS * a)
-            for a in range(2)
-        ]
+        lead_words = shared.tile([P, LEAD], U32, name="lead_words", align_bytes=64, offset=0)
+        rest_words = shared.tile([P, S - LEAD], U32, name="rest_words", align_bytes=64, offset=AT_DEALT)
+        passes = (
+            (lead_words[:], 0, LEAD),
+            (rest_words[:, :LEAD], LEAD, 2 * LEAD),
+            (rest_words[:, LEAD:], 2 * LEAD, S),
+        )
 
-        def quantise_weights(t):
-            if t < 2:
-                w_codes = keep.tile([P, P], U32, name=f"w_codes{t}", align_bytes=64)
+        def quantise_weights(u):
+            if u == 0:
+                w_codes = keep.tile([P, 2 * P], U32, name="w_codes0", align_bytes=64)
             else:
-                w_codes = shared.tile([P, P], U32, name=f"w_codes{t}", align_bytes=64, offset=4 * T + S * (t - 1))
-            w_scales = keep.tile([P, P], U8, name=f"w_scales{t}", align_bytes=64)
+                w_codes = shared.tile([P, 2 * P], U32, name="w_codes1", align_bytes=64, offset=AT_LEAD)
+            w_scales = keep.tile([P, 2 * P], U8, name=f"w_scales{u}", align_bytes=64)
             nc.vector.quantize_mx(
                 out=w_codes[:].bitcast(FP8X4),
                 scales=w_scales[:],
-                in_=w_bf16[t // 2][:, t % 2].rearrange("p m j -> p (m j)"),
+                in_=w_bf16[u][:].rearrange("p t m j -> p (t m j)"),
             )
-            return w_codes, w_scales
+            return [(w_codes[:, i * P : (i + 1) * P], w_scales[:, i * P : (i + 1) * P]) for i in range(2)]
 
-        def product(acc, weights, a):
-            nc.tensor.matmul_mx(
-                out=acc,
-                lhsT=weights[0][:].bitcast(FP8X4),
-                lhsT_scale=weights[1][:],
-                rhs=picked_words[a][:].bitcast(FP8X4),
-                rhs_scale=picked_scales[:, a * HS : (a + 1) * HS],
-                start=True,
-                stop=True,
+        def product(name, weights, some, result):
+            first = some[0][1]
+            acc = psum.tile([P, some[-1][2] - first], F32, name=name)
+            for words, s0, s1 in some:
+                nc.tensor.matmul_mx(
+                    out=acc[:, s0 - first : s1 - first],
+                    lhsT=weights[0].bitcast(FP8X4),
+                    lhsT_scale=weights[1],
+                    rhs=words.bitcast(FP8X4),
+                    rhs_scale=picked_scales[:, s0:s1],
+                    start=True,
+                    stop=True,
+                )
+            nc.scalar.copy(result, acc[:])
+
+        def scatter(t, result, s0, s1):
+            nc.vector.tensor_tensor(
+                placed[t][:].indirect(offsets[:, s0 // 16 : s1 // 16]), result, picked_scores[:, s0:s1], MULT
             )
 
         results = [keep.tile([P, S], F32, name=f"result{t}", align_bytes=64) for t in range(PACK)]
+        lead_result = shared.tile([P, LEAD], F32, name="lead_result", align_bytes=64, offset=AT_LEAD)
         weights = quantise_weights(0)
-        for a in range(2):
-            nc.vector.tensor_copy(
-                picked_words[a][:],
-                token_words[:].bitcast(U32).indirect(offsets[:, a * HS // 16 : (a + 1) * HS // 16]),
-            )
-            acc = psum.tile([P, HS], F32, name=f"acc0_{a}")
-            product(acc[:], weights, a)
-            nc.scalar.copy(results[0][:, a * HS : (a + 1) * HS], acc[:])
-        for t in range(1, PACK):
-            weights = quantise_weights(t)
-            acc = psum.tile([P, S], F32, name=f"acc{t}")
-            for a in range(2):
-                product(acc[:, a * HS : (a + 1) * HS], weights, a)
-            nc.scalar.copy(results[t][:], acc[:])
+        window = token_words[:].bitcast(U32)
+        nc.vector.tensor_copy(lead_words[:], window.indirect(offsets[:, : LEAD // 16]))
+        product("acc_lead", weights[0], passes[:1], lead_result[:])
+        nc.vector.tensor_copy(rest_words[:], window.indirect(offsets[:, LEAD // 16 :]))
+        product("acc0", weights[0], passes[1:], results[0][:, LEAD:])
+        product("acc1", weights[1], passes, results[1][:])
+        scatter(0, lead_result[:], 0, LEAD)
+        weights = quantise_weights(1)
+        for t in (2, 3):
+            product(f"acc{t}", weights[t - 2], passes, results[t][:])
 
         rounded = keep.tile([P, T * PACK], BF16, name="rounded", align_bytes=64)
         planes = rounded[:].rearrange("p (c t) -> p c t", t=PACK)
         split = 512
         out_rows = out_0.rearrange("(p t) c -> t p c", t=PACK)
         for t in range(PACK):
-            for s0, s1 in ((0, HS), (HS, S)) if t == 0 else ((0, S),):
-                nc.vector.tensor_tensor(
-                    placed[t][:].indirect(offsets[:, s0 // 16 : s1 // 16]),
-                    results[t][:, s0:s1],
-                    picked_scores[:, s0:s1],
-                    MULT,
-                )
+            s0 = LEAD if t == 0 else 0
+            scatter(t, results[t][:, s0:], s0, S)
             nc.sync.dma_start(out_rows[t], placed[t][:])
             if t < PACK - 2:
                 nc.scalar.copy(planes[:, :, t], placed[t][:])

@@ -160,7 +160,7 @@ def tile_picked_modgate_linnone_po_kernel(
 
         rounded = keep.tile([P, T * PACK], BF16, name="rounded", align_bytes=64)
         planes = rounded[:].rearrange("p (c t) -> p c t", t=PACK)
-        split = 512
+        split = 576
         out_rows = out_0.rearrange("(p t) c -> t p c", t=PACK)
         for t in range(PACK):
             s0 = LEAD if t == 0 else 0
@@ -173,20 +173,23 @@ def tile_picked_modgate_linnone_po_kernel(
                 nc.scalar.copy(planes[:, :split, t : t + 2], both)
                 nc.scalar.copy(planes[:, split:, t], placed[t][:, split:])
             else:
-                nc.vector.tensor_copy(planes[:, :split, t], placed[t][:, :split])
+                for c0, c1 in ((0, 256), (256, split)):
+                    nc.vector.tensor_copy(planes[:, c0:c1, t], placed[t][:, c0:c1])
                 for c0, c1 in ((split, 768), (768, T)):
                     nc.scalar.copy(planes[:, c0:c1, t], placed[t][:, c0:c1])
 
         out_scales = keep.tile([P, T], U8, name="out_scales", align_bytes=64)
         words_hbm = out_1[0].rearrange("p c r -> p (c r)").bitcast(I32)
-        for s0, s1 in ((split, 768), (0, split), (768, T)):
-            out_codes = keep.tile([P, s1 - s0], I32, name=f"out_codes{s0}", align_bytes=64)
-            nc.vector.quantize_mx(
-                out=out_codes[:].bitcast(FP8X4),
-                scales=out_scales[:, s0:s1],
-                in_=rounded[:, PACK * s0 : PACK * s1],
-            )
-            nc.sync.dma_start(words_hbm[:, s0:s1], out_codes[:])
+        for cuts in ((0, 256, 384), (384, 512, 768), (768, T)):
+            first = cuts[0]
+            out_codes = keep.tile([P, cuts[-1] - first], I32, name=f"out_codes{first}", align_bytes=64)
+            for s0, s1 in zip(cuts, cuts[1:]):
+                nc.vector.quantize_mx(
+                    out=out_codes[:, s0 - first : s1 - first].bitcast(FP8X4),
+                    scales=out_scales[:, s0:s1],
+                    in_=rounded[:, PACK * s0 : PACK * s1],
+                )
+            nc.sync.dma_start(words_hbm[:, first : cuts[-1]], out_codes[:])
         for q in range(4):
             queue = nc.scalar if q % 2 == 0 else nc.sync
             queue.dma_start(

@@ -68,7 +68,8 @@ def tile_picked_modgate_linnone_po_kernel(
         placed = []
         for t in range(PACK - 1):
             window = shared.tile([P, T], F32, name=f"placed{t}", align_bytes=64, offset=AT_PLACED + 4 * T * t)
-            nc.vector.memset(window[:].bitcast(I32), 0)
+            clear = nc.vector if t == 0 else nc.gpsimd
+            clear.memset(window[:].bitcast(I32), 0)
             placed.append(window)
         placed.append(placed[0])
 
@@ -103,19 +104,10 @@ def tile_picked_modgate_linnone_po_kernel(
                 deal(u, h)
         picked_scores = keep.tile([P, S], F32, name="picked_scores", align_bytes=64)
         nc.vector.tensor_copy(picked_scores[:], scores[:].indirect(offsets[:]))
-        lead_words = shared.tile([P, LEAD], U32, name="lead_words", align_bytes=64, offset=0)
-        rest_words = shared.tile([P, S - LEAD], U32, name="rest_words", align_bytes=64, offset=AT_DEALT)
-        passes = (
-            (lead_words[:], 0, LEAD),
-            (rest_words[:, :LEAD], LEAD, 2 * LEAD),
-            (rest_words[:, LEAD:], 2 * LEAD, S),
-        )
+        picked_words = shared.tile([P, S], U32, name="picked_words", align_bytes=64, offset=0)
 
         def quantise_weights(u):
-            if u == 0:
-                w_codes = keep.tile([P, 2 * P], U32, name="w_codes0", align_bytes=64)
-            else:
-                w_codes = shared.tile([P, 2 * P], U32, name="w_codes1", align_bytes=64, offset=AT_LEAD)
+            w_codes = keep.tile([P, 2 * P], U32, name=f"w_codes{u}", align_bytes=64)
             w_scales = keep.tile([P, 2 * P], U8, name=f"w_scales{u}", align_bytes=64)
             nc.vector.quantize_mx(
                 out=w_codes[:].bitcast(FP8X4),
@@ -124,19 +116,17 @@ def tile_picked_modgate_linnone_po_kernel(
             )
             return [(w_codes[:, i * P : (i + 1) * P], w_scales[:, i * P : (i + 1) * P]) for i in range(2)]
 
-        def product(name, weights, some, result):
-            first = some[0][1]
-            acc = psum.tile([P, some[-1][2] - first], F32, name=name)
-            for words, s0, s1 in some:
-                nc.tensor.matmul_mx(
-                    out=acc[:, s0 - first : s1 - first],
-                    lhsT=weights[0].bitcast(FP8X4),
-                    lhsT_scale=weights[1],
-                    rhs=words.bitcast(FP8X4),
-                    rhs_scale=picked_scales[:, s0:s1],
-                    start=True,
-                    stop=True,
-                )
+        def product(name, weights, s0, s1, result):
+            acc = psum.tile([P, s1 - s0], F32, name=name)
+            nc.tensor.matmul_mx(
+                out=acc[:],
+                lhsT=weights[0].bitcast(FP8X4),
+                lhsT_scale=weights[1],
+                rhs=picked_words[:, s0:s1].bitcast(FP8X4),
+                rhs_scale=picked_scales[:, s0:s1],
+                start=True,
+                stop=True,
+            )
             nc.scalar.copy(result, acc[:])
 
         def scatter(t, result, s0, s1):
@@ -145,22 +135,22 @@ def tile_picked_modgate_linnone_po_kernel(
             )
 
         results = [keep.tile([P, S], F32, name=f"result{t}", align_bytes=64) for t in range(PACK)]
-        lead_result = shared.tile([P, LEAD], F32, name="lead_result", align_bytes=64, offset=AT_LEAD)
+        lead_result = keep.tile([P, LEAD], F32, name="lead_result", align_bytes=64)
         weights = quantise_weights(0)
         window = token_words[:].bitcast(U32)
-        nc.vector.tensor_copy(lead_words[:], window.indirect(offsets[:, : LEAD // 16]))
-        product("acc_lead", weights[0], passes[:1], lead_result[:])
-        nc.vector.tensor_copy(rest_words[:], window.indirect(offsets[:, LEAD // 16 :]))
-        product("acc0", weights[0], passes[1:], results[0][:, LEAD:])
-        product("acc1", weights[1], passes, results[1][:])
+        for s0, s1 in ((0, LEAD), (LEAD, S - LEAD), (S - LEAD, S)):
+            nc.vector.tensor_copy(picked_words[:, s0:s1], window.indirect(offsets[:, s0 // 16 : s1 // 16]))
+            result = lead_result[:] if s0 == 0 else results[0][:, s0:s1]
+            product(f"acc0_{s0}", weights[0], s0, s1, result)
+        product("acc1", weights[1], 0, S, results[1][:])
         scatter(0, lead_result[:], 0, LEAD)
         weights = quantise_weights(1)
         for t in (2, 3):
-            product(f"acc{t}", weights[t - 2], passes, results[t][:])
+            product(f"acc{t}", weights[t - 2], 0, S, results[t][:])
 
         rounded = keep.tile([P, T * PACK], BF16, name="rounded", align_bytes=64)
         planes = rounded[:].rearrange("p (c t) -> p c t", t=PACK)
-        split = 576
+        split = 512
         out_rows = out_0.rearrange("(p t) c -> t p c", t=PACK)
         for t in range(PACK):
             s0 = LEAD if t == 0 else 0

@@ -104,17 +104,13 @@ def tile_picked_modgate_linnone_po_kernel(
                 deal(u, h)
         picked_scores = keep.tile([P, S], F32, name="picked_scores", align_bytes=64)
         nc.vector.tensor_copy(picked_scores[:], scores[:].indirect(offsets[:]))
-        picked_words = shared.tile([P, S], U32, name="picked_words", align_bytes=64, offset=0)
+        picked_words = keep.tile([P, S], U32, name="picked_words", align_bytes=64)
 
-        def quantise_weights(u):
-            w_codes = keep.tile([P, 2 * P], U32, name=f"w_codes{u}", align_bytes=64)
-            w_scales = keep.tile([P, 2 * P], U8, name=f"w_scales{u}", align_bytes=64)
-            nc.vector.quantize_mx(
-                out=w_codes[:].bitcast(FP8X4),
-                scales=w_scales[:],
-                in_=w_bf16[u][:].rearrange("p t m j -> p (t m j)"),
-            )
-            return [(w_codes[:, i * P : (i + 1) * P], w_scales[:, i * P : (i + 1) * P]) for i in range(2)]
+        def quantise_weights(name, dealt, planes, at):
+            w_codes = shared.tile([P, planes * P], U32, name=f"w_codes{name}", align_bytes=64, offset=at)
+            w_scales = keep.tile([P, planes * P], U8, name=f"w_scales{name}", align_bytes=64)
+            nc.vector.quantize_mx(out=w_codes[:].bitcast(FP8X4), scales=w_scales[:], in_=dealt)
+            return [(w_codes[:, i * P : (i + 1) * P], w_scales[:, i * P : (i + 1) * P]) for i in range(planes)]
 
         def product(name, weights, s0, s1, result):
             acc = psum.tile([P, s1 - s0], F32, name=name)
@@ -136,15 +132,16 @@ def tile_picked_modgate_linnone_po_kernel(
 
         results = [keep.tile([P, S], F32, name=f"result{t}", align_bytes=64) for t in range(PACK)]
         lead_result = keep.tile([P, LEAD], F32, name="lead_result", align_bytes=64)
-        weights = quantise_weights(0)
+        weights = quantise_weights(0, w_bf16[0][:, 0].rearrange("p m j -> p (m j)"), 1, AT_LEAD)
         window = token_words[:].bitcast(U32)
         for s0, s1 in ((0, LEAD), (LEAD, S - LEAD), (S - LEAD, S)):
             nc.vector.tensor_copy(picked_words[:, s0:s1], window.indirect(offsets[:, s0 // 16 : s1 // 16]))
             result = lead_result[:] if s0 == 0 else results[0][:, s0:s1]
-            product(f"acc0_{s0}", weights[0], s0, s1, result)
-        product("acc1", weights[1], 0, S, results[1][:])
+            product(f"acc0_{s1 - s0}", weights[0], s0, s1, result)
+        weights = quantise_weights(1, w_bf16[0][:, 1].rearrange("p m j -> p (m j)"), 1, AT_WORDS)
+        product(f"acc0_{S - 2 * LEAD}", weights[0], 0, S, results[1][:])
         scatter(0, lead_result[:], 0, LEAD)
-        weights = quantise_weights(1)
+        weights = quantise_weights(23, w_bf16[1][:].rearrange("p t m j -> p (t m j)"), 2, AT_LEAD)
         for t in (2, 3):
             product(f"acc{t}", weights[t - 2], 0, S, results[t][:])
 

@@ -71,7 +71,7 @@ def tile_picked_modgate_linnone_po_kernel(
             clear = nc.vector if t == 0 else nc.gpsimd
             clear.memset(window[:].bitcast(I32), 0)
             placed.append(window)
-        placed.append(placed[0])
+        placed = [placed[0]] + placed
 
         scores = shared.tile([P, T], F32, name="scores", align_bytes=64, offset=0)
         for b in range(2):
@@ -138,27 +138,27 @@ def tile_picked_modgate_linnone_po_kernel(
             nc.vector.tensor_copy(picked_words[:, s0:s1], window.indirect(offsets[:, s0 // 16 : s1 // 16]))
             result = lead_result[:] if s0 == 0 else results[0][:, s0:s1]
             product(f"acc0_{s1 - s0}", weights[0], s0, s1, result)
-        weights = quantise_weights(1, w_bf16[0][:, 1].rearrange("p m j -> p (m j)"), 1, AT_WORDS)
-        product(f"acc0_{S - 2 * LEAD}", weights[0], 0, S, results[1][:])
+        weights = quantise_weights(23, w_bf16[1][:].rearrange("p t m j -> p (t m j)"), 2, AT_LEAD + 4 * P)
+        product(f"acc0_{S - 2 * LEAD}", weights[0], 0, S, results[2][:])
+        product("acc3", weights[1], 0, S, results[3][:])
         scatter(0, lead_result[:], 0, LEAD)
-        weights = quantise_weights(23, w_bf16[1][:].rearrange("p t m j -> p (t m j)"), 2, AT_LEAD)
-        for t in (2, 3):
-            product(f"acc{t}", weights[t - 2], 0, S, results[t][:])
+        weights = quantise_weights(1, w_bf16[0][:, 1].rearrange("p m j -> p (m j)"), 1, AT_LEAD)
+        product("acc1", weights[0], 0, S, results[1][:])
 
         rounded = keep.tile([P, T * PACK], BF16, name="rounded", align_bytes=64)
         planes = rounded[:].rearrange("p (c t) -> p c t", t=PACK)
         split = 512
         out_rows = out_0.rearrange("(p t) c -> t p c", t=PACK)
-        for t in range(PACK):
+        for t in (0, 2, 3, 1):
             s0 = LEAD if t == 0 else 0
             scatter(t, results[t][:, s0:], s0, S)
             nc.sync.dma_start(out_rows[t], placed[t][:])
-            if t < PACK - 2:
-                nc.scalar.copy(planes[:, :, t], placed[t][:])
-            elif t == PACK - 2:
+            if t == 0:
                 both = placed[t][:, :split].unsqueeze(2).to_broadcast([P, split, 2])
                 nc.scalar.copy(planes[:, :split, t : t + 2], both)
                 nc.scalar.copy(planes[:, split:, t], placed[t][:, split:])
+            elif t > 1:
+                nc.scalar.copy(planes[:, :, t], placed[t][:])
             else:
                 for c0, c1 in ((0, 256), (256, split)):
                     nc.vector.tensor_copy(planes[:, c0:c1, t], placed[t][:, c0:c1])

@@ -68,8 +68,7 @@ def tile_picked_modgate_linnone_po_kernel(
         placed = []
         for t in range(PACK - 1):
             window = shared.tile([P, T], F32, name=f"placed{t}", align_bytes=64, offset=AT_PLACED + 4 * T * t)
-            clear = nc.vector if t == 0 else nc.gpsimd
-            clear.memset(window[:].bitcast(I32), 0)
+            nc.vector.memset(window[:].bitcast(I32), 0)
             placed.append(window)
         placed = [placed[0]] + placed
 

@@ -152,11 +152,7 @@ def tile_picked_modgate_linnone_po_kernel(
             s0 = LEAD if t == 0 else 0
             scatter(t, results[t][:, s0:], s0, S)
             nc.sync.dma_start(out_rows[t], placed[t][:])
-            if t == 0:
-                both = placed[t][:, :split].unsqueeze(2).to_broadcast([P, split, 2])
-                nc.scalar.copy(planes[:, :split, t : t + 2], both)
-                nc.scalar.copy(planes[:, split:, t], placed[t][:, split:])
-            elif t > 1:
+            if t != 1:
                 nc.scalar.copy(planes[:, :, t], placed[t][:])
             else:
                 for c0, c1 in ((0, 256), (256, split)):

@@ -50,11 +50,8 @@ def tile_picked_modgate_linnone_po_kernel(
         w_rows = w1.rearrange("(p j) c -> p j c", j=PACK)
         w_first = keep.tile([P, PACK, CUT], F32, name="w_first", align_bytes=64)
         nc.sync.dma_start(w_first[:], w_rows[:, :, :CUT])
-        for q in range(4):
-            nc.sync.dma_start(
-                token_scales[32 * q : 32 * q + 4, :].bitcast(I32),
-                x_scales[0, 4 * q : 4 * q + 4, :].bitcast(I32),
-            )
+        for r in range(4):
+            nc.sync.dma_start(token_scales[r:P:32, :].bitcast(I32), x_scales[0, r:16:4, :].bitcast(I32))
         w_raw = [(w_first, 0, CUT // PACK)]
         for c0 in (CUT,):
             raw = shared.tile(
@@ -157,12 +154,12 @@ def tile_picked_modgate_linnone_po_kernel(
             else:
                 for c0, c1 in ((0, 256), (256, split)):
                     nc.vector.tensor_copy(planes[:, c0:c1, t], placed[t][:, c0:c1])
-                for c0, c1 in ((split, 768), (768, T)):
+                for c0, c1 in ((split, 768), (768, 896), (896, T)):
                     nc.scalar.copy(planes[:, c0:c1, t], placed[t][:, c0:c1])
 
         out_scales = keep.tile([P, T], U8, name="out_scales", align_bytes=64)
         words_hbm = out_1[0].rearrange("p c r -> p (c r)").bitcast(I32)
-        for cuts in ((0, 256, 384), (384, 512, 768), (768, T)):
+        for cuts in ((0, 256, 384), (384, 512, 768), (768, 896, T)):
             first = cuts[0]
             out_codes = keep.tile([P, cuts[-1] - first], I32, name=f"out_codes{first}", align_bytes=64)
             for s0, s1 in zip(cuts, cuts[1:]):
@@ -172,9 +169,6 @@ def tile_picked_modgate_linnone_po_kernel(
                     in_=rounded[:, PACK * s0 : PACK * s1],
                 )
             nc.sync.dma_start(words_hbm[:, first : cuts[-1]], out_codes[:])
-        for q in range(4):
-            queue = nc.scalar if q % 2 == 0 else nc.sync
-            queue.dma_start(
-                out_2[0, 4 * q : 4 * q + 4, :].bitcast(I32),
-                out_scales[32 * q : 32 * q + 4, :].bitcast(I32),
-            )
+        for r in range(4):
+            queue = nc.scalar if r % 2 == 0 else nc.sync
+            queue.dma_start(out_2[0, r:16:4, :].bitcast(I32), out_scales[r:P:32, :].bitcast(I32))

@@ -170,5 +170,5 @@ def tile_picked_modgate_linnone_po_kernel(
                 )
             nc.sync.dma_start(words_hbm[:, first : cuts[-1]], out_codes[:])
         for r in range(4):
-            queue = nc.scalar if r % 2 == 0 else nc.sync
+            queue = nc.scalar if r == 0 else nc.sync
             queue.dma_start(out_2[0, r:16:4, :].bitcast(I32), out_scales[r:P:32, :].bitcast(I32))

@@ -13,18 +13,20 @@ U16 = mybir.dt.uint16
 U8 = mybir.dt.uint8
 FP8X4 = mybir.dt.float8_e4m3fn_x4
 MULT = mybir.AluOpType.mult
+ADD = mybir.AluOpType.add
+COPY = mybir.ActivationFunctionType.Copy
 
 P = 128
 PACK = 4
-CUT = 192
-REST = N - CUT
-AT_SCALES = 4 * T
-AT_WORDS = AT_SCALES + S
-AT_REST = AT_WORDS + 4 * T
-AT_PLACED = AT_REST + 4 * PACK * (N - CUT)
-AT_DEALT = AT_PLACED + 4 * T * (PACK - 1)
-AT_LEAD = AT_DEALT + 4 * T
 LEAD = 128
+SHARE = 224
+PIECE = 256
+AT_WINDOWS = 0
+AT_PICKED = AT_WINDOWS + 3 * 4 * T
+AT_DEALT = AT_PICKED + 5 * S
+AT_SCORES = AT_DEALT + 2 * 2 * N
+AT_RESULT = AT_SCORES + 4 * T
+AT_CODES = AT_RESULT + 4 * S
 
 
 def tile_picked_modgate_linnone_po_kernel(
@@ -36,40 +38,39 @@ def tile_picked_modgate_linnone_po_kernel(
         psum = ctx.enter_context(tc.psum_pool(name="psum", bufs=1))
         shared = ctx.enter_context(tc.tile_pool(name="shared", bufs=1))
 
-        score_cols = shared.tile([P, T // P], F32, name="score_cols", align_bytes=64, offset=AT_DEALT)
+        token_scales = keep.tile([P, T], U8, name="token_scales", align_bytes=64)
+        nc.vector.memset(token_scales[:].bitcast(I32), 0)
+        score_cols = keep.tile([P, T // P], F32, name="score_cols", align_bytes=64)
         nc.sync.dma_start(score_cols[:], gate[0].rearrange("(p j) -> p j", p=P))
         offsets = keep.tile([P, S // 16], U16, name="offsets")
         nc.sync.dma_start(offsets[:], offs)
-
-        token_scales = keep.tile([P, T], U8, name="token_scales", align_bytes=64)
-        nc.vector.memset(token_scales[:].bitcast(I32), 0)
-        identity = shared.tile([P, P], F32, name="identity", align_bytes=64, offset=AT_DEALT + 2 * T)
-        ramp = shared.tile([P, (AT_DEALT - AT_SCALES) // 4], F32, name="ramp", align_bytes=64, offset=AT_SCALES)
-        nc.gpsimd.iota(ramp[:, :P], [[1, P]], base=0, channel_multiplier=-1, allow_small_or_imprecise_dtypes=True)
-        nc.vector.tensor_scalar(identity[:], ramp[:, :P], 0.0, None, mybir.AluOpType.is_equal)
-        w_rows = w1.rearrange("(p j) c -> p j c", j=PACK)
-        w_first = keep.tile([P, PACK, CUT], F32, name="w_first", align_bytes=64)
-        nc.sync.dma_start(w_first[:], w_rows[:, :, :CUT])
+        token_words = keep.tile([P, T], I32, name="token_words", align_bytes=64)
+        nc.sync.dma_start(token_words[:], x_words[0].rearrange("p c r -> p (c r)").bitcast(I32))
         for r in range(4):
             nc.sync.dma_start(token_scales[r:P:32, :].bitcast(I32), x_scales[0, r:16:4, :].bitcast(I32))
-        w_raw = [(w_first, 0, CUT // PACK)]
-        for c0 in (CUT,):
-            raw = shared.tile(
-                [P, PACK, REST], F32, name=f"w_rest{c0}", align_bytes=64, offset=AT_REST + 4 * PACK * (c0 - CUT)
+        w_rows = w1.rearrange("(p j) c -> p j c", j=PACK)
+        w_raw = []
+        for h in range(2):
+            raw = keep.tile([P, 2, N], F32, name=f"w_raw{h}", align_bytes=64)
+            nc.sync.dma_start(raw[:], w_rows[:, 2 * h : 2 * h + 2, :])
+            w_raw.append(raw)
+
+        identity = keep.tile([P, P], F32, name="identity", align_bytes=64)
+        ramp = shared.tile([P, AT_SCORES // 4], F32, name="ramp", align_bytes=64, offset=AT_WINDOWS)
+        nc.gpsimd.iota(ramp[:, :P], [[1, P]], base=0, channel_multiplier=-1, allow_small_or_imprecise_dtypes=True)
+        nc.vector.tensor_scalar(identity[:], ramp[:, :P], 0.0, None, mybir.AluOpType.is_equal)
+
+        placed = {}
+        for t in (0,):
+            placed[t] = keep.tile([P, T], F32, name=f"placed{t}", align_bytes=64)
+            nc.vector.memset(placed[t][:].bitcast(I32), 0)
+        for t in (1, 3, 2):
+            placed[t] = shared.tile(
+                [P, T], F32, name=f"placed{t}", align_bytes=64, offset=AT_WINDOWS + 4 * T * (t - 1)
             )
-            nc.sync.dma_start(raw[:], w_rows[:, :, c0 : c0 + REST])
-            w_raw.append((raw, c0 // PACK, (c0 + REST) // PACK))
-        token_words = shared.tile([P, T], I32, name="token_words", align_bytes=64, offset=AT_WORDS)
-        nc.sync.dma_start(token_words[:], x_words[0].rearrange("p c r -> p (c r)").bitcast(I32))
+            nc.gpsimd.memset(placed[t][:].bitcast(I32), 0)
 
-        placed = []
-        for t in range(PACK - 1):
-            window = shared.tile([P, T], F32, name=f"placed{t}", align_bytes=64, offset=AT_PLACED + 4 * T * t)
-            nc.vector.memset(window[:].bitcast(I32), 0)
-            placed.append(window)
-        placed = [placed[0]] + placed
-
-        scores = shared.tile([P, T], F32, name="scores", align_bytes=64, offset=0)
+        scores = shared.tile([P, T], F32, name="scores", align_bytes=64, offset=AT_SCORES)
         for b in range(2):
             spread = psum.tile([P, PACK, P], F32, name=f"spread{b}")
             for j in range(PACK):
@@ -81,94 +82,112 @@ def tile_picked_modgate_linnone_po_kernel(
                 scores[:].rearrange("p (n j) -> p n j", j=T // P)[:, :, PACK * b : PACK * (b + 1)],
                 spread[:].rearrange("p j n -> p n j"),
             )
-
-        w_bf16 = [
-            shared.tile([P, 2, P, PACK], BF16, name=f"w_bf16_{u}", align_bytes=64, offset=AT_DEALT + 2 * u * T)
-            for u in range(2)
-        ]
-
-        def deal(u, h):
-            raw, m0, m1 = w_raw[h]
-            src = raw[:].rearrange("p j (m t) -> p m j t", t=PACK)[:, :, :, 2 * u : 2 * u + 2]
-            dst = w_bf16[u][:].rearrange("p t m j -> p m j t")[:, m0:m1]
-            nc.scalar.copy(dst, src)
-
-        picked_scales = shared.tile([P, S], U8, name="picked_scales", align_bytes=64, offset=AT_SCALES)
-        nc.vector.tensor_copy(picked_scales[:], token_scales[:].indirect(offsets[:]))
-        for u in range(2):
-            for h in range(2):
-                deal(u, h)
         picked_scores = keep.tile([P, S], F32, name="picked_scores", align_bytes=64)
-        nc.vector.tensor_copy(picked_scores[:], scores[:].indirect(offsets[:]))
-        picked_words = keep.tile([P, S], U32, name="picked_words", align_bytes=64)
+        nc.scalar.activation(picked_scores[:], scores[:].indirect(offsets[:]), COPY)
 
-        def quantise_weights(name, dealt, planes, at):
-            w_codes = shared.tile([P, planes * P], U32, name=f"w_codes{name}", align_bytes=64, offset=at)
-            w_scales = keep.tile([P, planes * P], U8, name=f"w_scales{name}", align_bytes=64)
-            nc.vector.quantize_mx(out=w_codes[:].bitcast(FP8X4), scales=w_scales[:], in_=dealt)
-            return [(w_codes[:, i * P : (i + 1) * P], w_scales[:, i * P : (i + 1) * P]) for i in range(planes)]
+        picked_scales = shared.tile([P, S], U8, name="picked_scales", align_bytes=64, offset=AT_PICKED)
+        picked_words = shared.tile([P, S], U32, name="picked_words", align_bytes=64, offset=AT_PICKED + S)
+        nc.vector.tensor_copy(picked_words[:], token_words[:].bitcast(U32).indirect(offsets[:]))
+        nc.vector.tensor_copy(picked_scales[:], token_scales[:].indirect(offsets[:]))
 
-        def product(name, weights, s0, s1, result):
+        pairs = {"outer": slice(0, 4, 3), "inner": slice(1, 3)}
+        dealt = {
+            u: shared.tile([P, 2, P, PACK], BF16, name=f"dealt_{u}", align_bytes=64, offset=AT_DEALT + 4 * N * i)
+            for i, u in enumerate(pairs)
+        }
+
+        def deal(copy, u, h):
+            src = w_raw[h][:].rearrange("p j (m t) -> p m j t", t=PACK)[:, :, :, pairs[u]]
+            dst = dealt[u][:].rearrange("p t m j -> p m j t")[:, :, 2 * h : 2 * h + 2, :]
+            copy(dst, src)
+
+        deal(nc.vector.tensor_copy, "outer", 0)
+        deal(nc.vector.tensor_copy, "outer", 1)
+
+        weights = {}
+        for u, planes in (("outer", (0, 3)), ("inner", (1, 2))):
+            if u == "inner":
+                deal(nc.vector.tensor_copy, u, 0)
+                deal(nc.scalar.copy, u, 1)
+            at = AT_CODES + (4 * S if u == "outer" else 0)
+            w_codes = shared.tile([P, 2 * P], U32, name=f"w_codes_{u}", align_bytes=64, offset=at)
+            w_scales = keep.tile([P, 2 * P], U8, name=f"w_scales_{u}", align_bytes=64)
+            nc.vector.quantize_mx(
+                out=w_codes[:].bitcast(FP8X4),
+                scales=w_scales[:],
+                in_=dealt[u][:].rearrange("p t m j -> p (t m j)"),
+            )
+            for i, t in enumerate(planes):
+                weights[t] = (w_codes[:, i * P : (i + 1) * P], w_scales[:, i * P : (i + 1) * P])
+
+        def product(name, t, s0, s1):
             acc = psum.tile([P, s1 - s0], F32, name=name)
             nc.tensor.matmul_mx(
                 out=acc[:],
-                lhsT=weights[0].bitcast(FP8X4),
-                lhsT_scale=weights[1],
+                lhsT=weights[t][0].bitcast(FP8X4),
+                lhsT_scale=weights[t][1],
                 rhs=picked_words[:, s0:s1].bitcast(FP8X4),
                 rhs_scale=picked_scales[:, s0:s1],
                 start=True,
                 stop=True,
             )
-            nc.scalar.copy(result, acc[:])
+            return acc
 
-        def scatter(t, result, s0, s1):
-            nc.vector.tensor_tensor(
-                placed[t][:].indirect(offsets[:, s0 // 16 : s1 // 16]), result, picked_scores[:, s0:s1], MULT
-            )
+        def weigh(pool, name, acc, a0, s0, s1, **place):
+            result = pool.tile([P, s1 - s0], F32, name=name, align_bytes=64, **place)
+            nc.vector.tensor_tensor(result[:], acc[:, s0 - a0 : s1 - a0], picked_scores[:, s0:s1], MULT)
+            return result
 
-        results = [keep.tile([P, S], F32, name=f"result{t}", align_bytes=64) for t in range(PACK)]
-        lead_result = keep.tile([P, LEAD], F32, name="lead_result", align_bytes=64)
-        weights = quantise_weights(0, w_bf16[0][:, 0].rearrange("p m j -> p (m j)"), 1, AT_LEAD)
-        window = token_words[:].bitcast(U32)
-        for s0, s1 in ((0, LEAD), (LEAD, S - LEAD), (S - LEAD, S)):
-            nc.vector.tensor_copy(picked_words[:, s0:s1], window.indirect(offsets[:, s0 // 16 : s1 // 16]))
-            result = lead_result[:] if s0 == 0 else results[0][:, s0:s1]
-            product(f"acc0_{s1 - s0}", weights[0], s0, s1, result)
-        weights = quantise_weights(23, w_bf16[1][:].rearrange("p t m j -> p (t m j)"), 2, AT_LEAD + 4 * P)
-        product(f"acc0_{S - 2 * LEAD}", weights[0], 0, S, results[2][:])
-        product("acc3", weights[1], 0, S, results[3][:])
-        scatter(0, lead_result[:], 0, LEAD)
-        weights = quantise_weights(1, w_bf16[0][:, 1].rearrange("p m j -> p (m j)"), 1, AT_LEAD)
-        product("acc1", weights[0], 0, S, results[1][:])
+        def target(t, s0, s1):
+            return placed[t][:].indirect(offsets[:, s0 // 16 : s1 // 16])
 
-        rounded = keep.tile([P, T * PACK], BF16, name="rounded", align_bytes=64)
-        planes = rounded[:].rearrange("p (c t) -> p c t", t=PACK)
-        split = 512
+        first = [(s0, s1, product(f"acc0_{s0}", 0, s0, s1)) for s0, s1 in ((0, LEAD), (LEAD, 2 * LEAD), (2 * LEAD, S))]
+        acc = {t: product(f"acc{t}", t, 0, S) for t in (3, 2, 1)}
+
         out_rows = out_0.rearrange("(p t) c -> t p c", t=PACK)
-        for t in (0, 2, 3, 1):
-            s0 = LEAD if t == 0 else 0
-            scatter(t, results[t][:, s0:], s0, S)
-            nc.sync.dma_start(out_rows[t], placed[t][:])
-            if t != 1:
-                nc.scalar.copy(planes[:, :, t], placed[t][:])
-            else:
-                for c0, c1 in ((0, 256), (256, split)):
-                    nc.vector.tensor_copy(planes[:, c0:c1, t], placed[t][:, c0:c1])
-                for c0, c1 in ((split, 768), (768, 896), (896, T)):
-                    nc.scalar.copy(planes[:, c0:c1, t], placed[t][:, c0:c1])
+        for s0, s1, a in first:
+            result = weigh(keep, f"result0_{s0}", a, s0, s0, s1)
+            nc.scalar.activation(target(0, s0, s1), result[:], COPY)
+        nc.sync.dma_start(out_rows[0], placed[0][:])
+        result = weigh(keep, "result3_a", acc[3], 0, 0, SHARE)
+        nc.scalar.activation(target(3, 0, SHARE), result[:], COPY)
+        result = weigh(keep, "result2_a", acc[2], 0, 0, S - LEAD)
+        nc.scalar.activation(target(2, 0, S - LEAD), result[:], COPY)
+        result1 = weigh(shared, "result1", acc[1], 0, 0, S, offset=AT_RESULT)
+        result3 = weigh(shared, "result3_b", acc[3], 0, SHARE, S, offset=AT_CODES)
+        nc.vector.tensor_copy(target(1, 0, S), result1[:])
+        nc.sync.dma_start(out_rows[1], placed[1][:])
+        nc.vector.tensor_copy(target(3, SHARE, S), result3[:])
+        nc.sync.dma_start(out_rows[3], placed[3][:])
+        result = weigh(shared, "result2_b", acc[2], 0, S - LEAD, S, offset=AT_RESULT)
+        nc.scalar.activation(target(2, S - LEAD, S), result[:], COPY)
+        nc.sync.dma_start(out_rows[2], placed[2][:])
+
+        pieces = range(0, T, PIECE)
+        paired = {c: keep.tile([P, 2, PIECE, 2], BF16, name=f"paired{c}", align_bytes=64) for c in pieces}
+        for t in (0, 1):
+            for c in pieces:
+                nc.gpsimd.tensor_scalar(paired[c][:, 0, :, t], placed[t][:, c : c + PIECE], 1.0, 0.0, MULT, ADD)
+        for t in (3, 2):
+            for c in pieces:
+                nc.vector.tensor_copy(paired[c][:, 1, :, t - 2], placed[t][:, c : c + PIECE])
 
         out_scales = keep.tile([P, T], U8, name="out_scales", align_bytes=64)
         words_hbm = out_1[0].rearrange("p c r -> p (c r)").bitcast(I32)
-        for cuts in ((0, 256, 384), (384, 512, 768), (768, 896, T)):
-            first = cuts[0]
-            out_codes = keep.tile([P, cuts[-1] - first], I32, name=f"out_codes{first}", align_bytes=64)
-            for s0, s1 in zip(cuts, cuts[1:]):
-                nc.vector.quantize_mx(
-                    out=out_codes[:, s0 - first : s1 - first].bitcast(FP8X4),
-                    scales=out_scales[:, s0:s1],
-                    in_=rounded[:, PACK * s0 : PACK * s1],
-                )
-            nc.sync.dma_start(words_hbm[:, first : cuts[-1]], out_codes[:])
+        rounded = {}
+        for c in pieces:
+            rounded[c] = keep.tile([P, PACK * PIECE], BF16, name=f"rounded{c}", align_bytes=64)
+            copy, word = (nc.vector.tensor_copy, I32) if c == pieces[-1] else (nc.scalar.copy, U32)
+            copy(
+                rounded[c][:].bitcast(word).rearrange("p (c u) -> p c u", u=2),
+                paired[c][:].rearrange("p u c e -> p u (c e)").bitcast(word).rearrange("p u c -> p c u"),
+            )
+        for c in (pieces[0], pieces[1], pieces[3], pieces[2]):
+            out_codes = keep.tile([P, PIECE], I32, name=f"out_codes{c}", align_bytes=64)
+            nc.vector.quantize_mx(
+                out=out_codes[:].bitcast(FP8X4), scales=out_scales[:, c : c + PIECE], in_=rounded[c][:]
+            )
+            nc.sync.dma_start(words_hbm[:, c : c + PIECE], out_codes[:])
         for r in range(4):
             queue = nc.scalar if r == 0 else nc.sync
             queue.dma_start(out_2[0, r:16:4, :].bitcast(I32), out_scales[r:P:32, :].bitcast(I32))

@@ -19,14 +19,14 @@ COPY = mybir.ActivationFunctionType.Copy
 P = 128
 PACK = 4
 LEAD = 128
+HALF = S // 2
 SHARE = 224
 PIECE = 256
 AT_WINDOWS = 0
-AT_PICKED = AT_WINDOWS + 3 * 4 * T
-AT_DEALT = AT_PICKED + 5 * S
-AT_SCORES = AT_DEALT + 2 * 2 * N
-AT_RESULT = AT_SCORES + 4 * T
-AT_CODES = AT_RESULT + 4 * S
+AT_RAW = AT_WINDOWS + PACK * 4 * T
+AT_PICKED = AT_RAW + 4 * PACK * N
+AT_EARLY = AT_PICKED + 5 * S
+AT_LATE = AT_EARLY + 4 * N
 
 
 def tile_picked_modgate_linnone_po_kernel(
@@ -40,37 +40,35 @@ def tile_picked_modgate_linnone_po_kernel(
 
         token_scales = keep.tile([P, T], U8, name="token_scales", align_bytes=64)
         nc.vector.memset(token_scales[:].bitcast(I32), 0)
-        score_cols = keep.tile([P, T // P], F32, name="score_cols", align_bytes=64)
-        nc.sync.dma_start(score_cols[:], gate[0].rearrange("(p j) -> p j", p=P))
+        score_home = shared.tile([P, 2 * N], F32, name="score_cols", align_bytes=64, offset=AT_EARLY)
+        score_cols = score_home[:, : T // P]
+        nc.sync.dma_start(score_cols, gate[0].rearrange("(p j) -> p j", p=P))
         offsets = keep.tile([P, S // 16], U16, name="offsets")
         nc.sync.dma_start(offsets[:], offs)
         token_words = keep.tile([P, T], I32, name="token_words", align_bytes=64)
         nc.sync.dma_start(token_words[:], x_words[0].rearrange("p c r -> p (c r)").bitcast(I32))
         for r in range(4):
             nc.sync.dma_start(token_scales[r:P:32, :].bitcast(I32), x_scales[0, r:16:4, :].bitcast(I32))
-        w_rows = w1.rearrange("(p j) c -> p j c", j=PACK)
-        w_raw = []
-        for h in range(2):
-            raw = keep.tile([P, 2, N], F32, name=f"w_raw{h}", align_bytes=64)
-            nc.sync.dma_start(raw[:], w_rows[:, 2 * h : 2 * h + 2, :])
-            w_raw.append(raw)
 
         identity = keep.tile([P, P], F32, name="identity", align_bytes=64)
-        ramp = shared.tile([P, AT_SCORES // 4], F32, name="ramp", align_bytes=64, offset=AT_WINDOWS)
+        ramp = shared.tile([P, AT_EARLY // 4], F32, name="ramp", align_bytes=64, offset=AT_WINDOWS)
         nc.gpsimd.iota(ramp[:, :P], [[1, P]], base=0, channel_multiplier=-1, allow_small_or_imprecise_dtypes=True)
         nc.vector.tensor_scalar(identity[:], ramp[:, :P], 0.0, None, mybir.AluOpType.is_equal)
 
-        placed = {}
-        for t in (0,):
-            placed[t] = keep.tile([P, T], F32, name=f"placed{t}", align_bytes=64)
-            nc.vector.memset(placed[t][:].bitcast(I32), 0)
-        for t in (1, 3, 2):
-            placed[t] = shared.tile(
-                [P, T], F32, name=f"placed{t}", align_bytes=64, offset=AT_WINDOWS + 4 * T * (t - 1)
-            )
-            nc.gpsimd.memset(placed[t][:].bitcast(I32), 0)
+        w_rows = w1.rearrange("(p j) c -> p j c", j=PACK)
+        w_raw = []
+        for h in range(2):
+            raw = shared.tile([P, 2, N], F32, name=f"w_raw{h}", align_bytes=64, offset=AT_RAW + 8 * N * h)
+            nc.sync.dma_start(raw[:], w_rows[:, 2 * h : 2 * h + 2, :])
+            w_raw.append(raw)
 
-        scores = shared.tile([P, T], F32, name="scores", align_bytes=64, offset=AT_SCORES)
+        placed = {}
+        for t in (0, 1, 3, 2):
+            placed[t] = shared.tile([P, T], F32, name=f"placed{t}", align_bytes=64, offset=AT_WINDOWS + 4 * T * t)
+            engine = nc.vector if t == 0 else nc.gpsimd
+            engine.memset(placed[t][:].bitcast(I32), 0)
+
+        scores = keep.tile([P, T], F32, name="scores", align_bytes=64)
         for b in range(2):
             spread = psum.tile([P, PACK, P], F32, name=f"spread{b}")
             for j in range(PACK):
@@ -82,85 +80,88 @@ def tile_picked_modgate_linnone_po_kernel(
                 scores[:].rearrange("p (n j) -> p n j", j=T // P)[:, :, PACK * b : PACK * (b + 1)],
                 spread[:].rearrange("p j n -> p n j"),
             )
-        picked_scores = keep.tile([P, S], F32, name="picked_scores", align_bytes=64)
-        nc.scalar.activation(picked_scores[:], scores[:].indirect(offsets[:]), COPY)
 
         picked_scales = shared.tile([P, S], U8, name="picked_scales", align_bytes=64, offset=AT_PICKED)
         picked_words = shared.tile([P, S], U32, name="picked_words", align_bytes=64, offset=AT_PICKED + S)
         nc.vector.tensor_copy(picked_words[:], token_words[:].bitcast(U32).indirect(offsets[:]))
         nc.vector.tensor_copy(picked_scales[:], token_scales[:].indirect(offsets[:]))
 
-        pairs = {"outer": slice(0, 4, 3), "inner": slice(1, 3)}
-        dealt = {
-            u: shared.tile([P, 2, P, PACK], BF16, name=f"dealt_{u}", align_bytes=64, offset=AT_DEALT + 4 * N * i)
-            for i, u in enumerate(pairs)
-        }
+        dealt = [
+            shared.tile([P, 2, P, PACK], BF16, name=f"dealt{u}", align_bytes=64, offset=at)
+            for u, at in enumerate((AT_EARLY, AT_LATE))
+        ]
 
         def deal(copy, u, h):
-            src = w_raw[h][:].rearrange("p j (m t) -> p m j t", t=PACK)[:, :, :, pairs[u]]
+            src = w_raw[h][:].rearrange("p j (m t) -> p m j t", t=PACK)[:, :, :, 2 * u : 2 * u + 2]
             dst = dealt[u][:].rearrange("p t m j -> p m j t")[:, :, 2 * h : 2 * h + 2, :]
             copy(dst, src)
 
-        deal(nc.vector.tensor_copy, "outer", 0)
-        deal(nc.vector.tensor_copy, "outer", 1)
-
         weights = {}
-        for u, planes in (("outer", (0, 3)), ("inner", (1, 2))):
-            if u == "inner":
-                deal(nc.vector.tensor_copy, u, 0)
-                deal(nc.scalar.copy, u, 1)
-            at = AT_CODES + (4 * S if u == "outer" else 0)
-            w_codes = shared.tile([P, 2 * P], U32, name=f"w_codes_{u}", align_bytes=64, offset=at)
-            w_scales = keep.tile([P, 2 * P], U8, name=f"w_scales_{u}", align_bytes=64)
-            nc.vector.quantize_mx(
-                out=w_codes[:].bitcast(FP8X4),
-                scales=w_scales[:],
-                in_=dealt[u][:].rearrange("p t m j -> p (t m j)"),
-            )
-            for i, t in enumerate(planes):
-                weights[t] = (w_codes[:, i * P : (i + 1) * P], w_scales[:, i * P : (i + 1) * P])
 
-        def product(name, t, s0, s1):
-            acc = psum.tile([P, s1 - s0], F32, name=name)
-            nc.tensor.matmul_mx(
-                out=acc[:],
-                lhsT=weights[t][0].bitcast(FP8X4),
-                lhsT_scale=weights[t][1],
-                rhs=picked_words[:, s0:s1].bitcast(FP8X4),
-                rhs_scale=picked_scales[:, s0:s1],
-                start=True,
-                stop=True,
+        def quantise_weights(first, count, **place):
+            pool = shared if place else keep
+            codes = pool.tile([P, count * P], U32, name=f"w_codes{first}", align_bytes=64, **place)
+            scales = keep.tile([P, count * P], U8, name=f"w_scales{first}", align_bytes=64)
+            source = dealt[first // 2][:, first % 2 : first % 2 + count]
+            nc.vector.quantize_mx(
+                out=codes[:].bitcast(FP8X4), scales=scales[:], in_=source.rearrange("p t m j -> p (t m j)")
             )
+            for i in range(count):
+                weights[first + i] = (codes[:, i * P : (i + 1) * P], scales[:, i * P : (i + 1) * P])
+
+        def product(t, *cuts):
+            acc = psum.tile([P, cuts[-1] - cuts[0]], F32, name=f"acc{t}_{cuts[0]}")
+            for s0, s1 in zip(cuts, cuts[1:]):
+                nc.tensor.matmul_mx(
+                    out=acc[:, s0 - cuts[0] : s1 - cuts[0]],
+                    lhsT=weights[t][0].bitcast(FP8X4),
+                    lhsT_scale=weights[t][1],
+                    rhs=picked_words[:, s0:s1].bitcast(FP8X4),
+                    rhs_scale=picked_scales[:, s0:s1],
+                    start=True,
+                    stop=True,
+                )
             return acc
 
-        def weigh(pool, name, acc, a0, s0, s1, **place):
-            result = pool.tile([P, s1 - s0], F32, name=name, align_bytes=64, **place)
-            nc.vector.tensor_tensor(result[:], acc[:, s0 - a0 : s1 - a0], picked_scores[:, s0:s1], MULT)
+        def weigh(t, s0, s1, sums):
+            result = keep.tile([P, s1 - s0], F32, name=f"result{t}_{s0}", align_bytes=64)
+            nc.vector.tensor_tensor(result[:], sums, picked_scores[:, s0:s1], MULT)
             return result
 
         def target(t, s0, s1):
             return placed[t][:].indirect(offsets[:, s0 // 16 : s1 // 16])
 
-        first = [(s0, s1, product(f"acc0_{s0}", 0, s0, s1)) for s0, s1 in ((0, LEAD), (LEAD, 2 * LEAD), (2 * LEAD, S))]
-        acc = {t: product(f"acc{t}", t, 0, S) for t in (3, 2, 1)}
+        deal(nc.scalar.copy, 0, 0)
+        deal(nc.vector.tensor_copy, 0, 1)
+        picked_scores = keep.tile([P, S], F32, name="picked_scores", align_bytes=64)
+        nc.scalar.activation(picked_scores[:], scores[:].indirect(offsets[:]), COPY)
+        quantise_weights(0, 1)
+        quantise_weights(1, 1)
+        lead = product(0, 0, LEAD)
+        rest = product(0, LEAD, HALF, S)
+        whole = {1: product(1, 0, S)}
+        deal(nc.vector.tensor_copy, 1, 0)
+        deal(nc.scalar.copy, 1, 1)
 
         out_rows = out_0.rearrange("(p t) c -> t p c", t=PACK)
-        for s0, s1, a in first:
-            result = weigh(keep, f"result0_{s0}", a, s0, s0, s1)
-            nc.scalar.activation(target(0, s0, s1), result[:], COPY)
+        nc.scalar.activation(target(0, 0, LEAD), weigh(0, 0, LEAD, lead[:])[:], COPY)
+        quantise_weights(2, 2)
+        for t in (3, 2):
+            whole[t] = product(t, 0, S)
+        nc.scalar.activation(target(0, LEAD, S), weigh(0, LEAD, S, rest[:])[:], COPY)
         nc.sync.dma_start(out_rows[0], placed[0][:])
-        result = weigh(keep, "result3_a", acc[3], 0, 0, SHARE)
-        nc.scalar.activation(target(3, 0, SHARE), result[:], COPY)
-        result = weigh(keep, "result2_a", acc[2], 0, 0, S - LEAD)
-        nc.scalar.activation(target(2, 0, S - LEAD), result[:], COPY)
-        result1 = weigh(shared, "result1", acc[1], 0, 0, S, offset=AT_RESULT)
-        result3 = weigh(shared, "result3_b", acc[3], 0, SHARE, S, offset=AT_CODES)
-        nc.vector.tensor_copy(target(1, 0, S), result1[:])
+        result1 = weigh(1, 0, S, whole[1][:])
+        result3 = weigh(3, 0, SHARE, whole[3][:, :SHARE])
+        nc.vector.tensor_copy(target(1, 0, HALF), result1[:, :HALF])
+        result2 = weigh(2, 0, S, whole[2][:])
+        nc.scalar.activation(target(3, 0, SHARE), result3[:], COPY)
+        nc.scalar.activation(target(2, 0, S - LEAD), result2[:, : S - LEAD], COPY)
+        nc.scalar.activation(target(2, S - LEAD, S), result2[:, S - LEAD :], COPY)
+        result3 = weigh(3, SHARE, S, whole[3][:, SHARE:])
+        nc.vector.tensor_copy(target(1, HALF, S), result1[:, HALF:])
         nc.sync.dma_start(out_rows[1], placed[1][:])
         nc.vector.tensor_copy(target(3, SHARE, S), result3[:])
         nc.sync.dma_start(out_rows[3], placed[3][:])
-        result = weigh(shared, "result2_b", acc[2], 0, S - LEAD, S, offset=AT_RESULT)
-        nc.scalar.activation(target(2, S - LEAD, S), result[:], COPY)
         nc.sync.dma_start(out_rows[2], placed[2][:])
 
         pieces = range(0, T, PIECE)

@@ -20,8 +20,8 @@ P = 128
 PACK = 4
 LEAD = 128
 HALF = S // 2
-SHARE = 224
-PIECE = 256
+SHARE = 192
+CUTS = (0, 128, 384, 640, 768, T)
 AT_WINDOWS = 0
 AT_RAW = AT_WINDOWS + PACK * 4 * T
 AT_PICKED = AT_RAW + 4 * PACK * N
@@ -150,45 +150,44 @@ def tile_picked_modgate_linnone_po_kernel(
             whole[t] = product(t, 0, S)
         nc.scalar.activation(target(0, LEAD, S), weigh(0, LEAD, S, rest[:])[:], COPY)
         nc.sync.dma_start(out_rows[0], placed[0][:])
-        result1 = weigh(1, 0, S, whole[1][:])
-        result3 = weigh(3, 0, SHARE, whole[3][:, :SHARE])
-        nc.vector.tensor_copy(target(1, 0, HALF), result1[:, :HALF])
-        result2 = weigh(2, 0, S, whole[2][:])
-        nc.scalar.activation(target(3, 0, SHARE), result3[:], COPY)
-        nc.scalar.activation(target(2, 0, S - LEAD), result2[:, : S - LEAD], COPY)
-        nc.scalar.activation(target(2, S - LEAD, S), result2[:, S - LEAD :], COPY)
-        result3 = weigh(3, SHARE, S, whole[3][:, SHARE:])
-        nc.vector.tensor_copy(target(1, HALF, S), result1[:, HALF:])
+        result = {t: weigh(t, 0, S, whole[t][:]) for t in (1, 3, 2)}
+        nc.scalar.activation(target(3, 0, SHARE), result[3][:, :SHARE], COPY)
+        for s0, s1 in ((0, S - LEAD), (S - LEAD, S)):
+            nc.scalar.activation(target(2, s0, s1), result[2][:, s0:s1], COPY)
+        nc.vector.tensor_copy(target(1, 0, S), result[1][:])
         nc.sync.dma_start(out_rows[1], placed[1][:])
-        nc.vector.tensor_copy(target(3, SHARE, S), result3[:])
+        nc.vector.tensor_copy(target(3, SHARE, S), result[3][:, SHARE:])
         nc.sync.dma_start(out_rows[3], placed[3][:])
         nc.sync.dma_start(out_rows[2], placed[2][:])
 
-        pieces = range(0, T, PIECE)
-        paired = {c: keep.tile([P, 2, PIECE, 2], BF16, name=f"paired{c}", align_bytes=64) for c in pieces}
+        paired = keep.tile([P, 2, T, 2], BF16, name="paired", align_bytes=64)
         for t in (0, 1):
-            for c in pieces:
-                nc.gpsimd.tensor_scalar(paired[c][:, 0, :, t], placed[t][:, c : c + PIECE], 1.0, 0.0, MULT, ADD)
-        for t in (3, 2):
-            for c in pieces:
-                nc.vector.tensor_copy(paired[c][:, 1, :, t - 2], placed[t][:, c : c + PIECE])
+            nc.gpsimd.tensor_scalar(paired[:, 0, :, t], placed[t][:], 1.0, 0.0, MULT, ADD)
+        nc.vector.tensor_copy(paired[:, 1, :, 1], placed[3][:])
+        pieces = list(zip(CUTS, CUTS[1:]))
+        for c0, c1 in pieces:
+            nc.vector.tensor_copy(paired[:, 1, c0:c1, 0], placed[2][:, c0:c1])
 
         out_scales = keep.tile([P, T], U8, name="out_scales", align_bytes=64)
         words_hbm = out_1[0].rearrange("p c r -> p (c r)").bitcast(I32)
         rounded = {}
-        for c in pieces:
-            rounded[c] = keep.tile([P, PACK * PIECE], BF16, name=f"rounded{c}", align_bytes=64)
-            copy, word = (nc.vector.tensor_copy, I32) if c == pieces[-1] else (nc.scalar.copy, U32)
+        for c0, c1 in pieces:
+            rounded[c0] = keep.tile([P, PACK * (c1 - c0)], BF16, name=f"rounded{c0}", align_bytes=64)
+            copy, word = (nc.vector.tensor_copy, I32) if c1 == T else (nc.scalar.copy, U32)
             copy(
-                rounded[c][:].bitcast(word).rearrange("p (c u) -> p c u", u=2),
-                paired[c][:].rearrange("p u c e -> p u (c e)").bitcast(word).rearrange("p u c -> p c u"),
+                rounded[c0][:].bitcast(word).rearrange("p (c u) -> p c u", u=2),
+                paired[:, :, c0:c1].rearrange("p u c e -> p u (c e)").bitcast(word).rearrange("p u c -> p c u"),
             )
-        for c in (pieces[0], pieces[1], pieces[3], pieces[2]):
-            out_codes = keep.tile([P, PIECE], I32, name=f"out_codes{c}", align_bytes=64)
-            nc.vector.quantize_mx(
-                out=out_codes[:].bitcast(FP8X4), scales=out_scales[:, c : c + PIECE], in_=rounded[c][:]
-            )
-            nc.sync.dma_start(words_hbm[:, c : c + PIECE], out_codes[:])
+        for group in (pieces[:2], pieces[2:3], pieces[4:], pieces[3:4]):
+            first, last = min(group)[0], max(group)[1]
+            out_codes = keep.tile([P, last - first], I32, name=f"out_codes{first}", align_bytes=64)
+            for c0, c1 in group:
+                nc.vector.quantize_mx(
+                    out=out_codes[:, c0 - first : c1 - first].bitcast(FP8X4),
+                    scales=out_scales[:, c0:c1],
+                    in_=rounded[c0][:],
+                )
+            nc.sync.dma_start(words_hbm[:, first:last], out_codes[:])
         for r in range(4):
             queue = nc.scalar if r == 0 else nc.sync
             queue.dma_start(out_2[0, r:16:4, :].bitcast(I32), out_scales[r:P:32, :].bitcast(I32))

@@ -20,13 +20,12 @@ P = 128
 PACK = 4
 LEAD = 128
 HALF = S // 2
-SHARE = 192
-CUTS = (0, 128, 384, 640, 768, T)
+SHARE = 256
+CUTS = (0, 128, 384, 640, 896, T)
 AT_WINDOWS = 0
 AT_RAW = AT_WINDOWS + PACK * 4 * T
 AT_PICKED = AT_RAW + 4 * PACK * N
 AT_EARLY = AT_PICKED + 5 * S
-AT_LATE = AT_EARLY + 4 * N
 
 
 def tile_picked_modgate_linnone_po_kernel(
@@ -40,7 +39,7 @@ def tile_picked_modgate_linnone_po_kernel(
 
         token_scales = keep.tile([P, T], U8, name="token_scales", align_bytes=64)
         nc.vector.memset(token_scales[:].bitcast(I32), 0)
-        score_home = shared.tile([P, 2 * N], F32, name="score_cols", align_bytes=64, offset=AT_EARLY)
+        score_home = shared.tile([P, N], F32, name="score_cols", align_bytes=64, offset=AT_EARLY)
         score_cols = score_home[:, : T // P]
         nc.sync.dma_start(score_cols, gate[0].rearrange("(p j) -> p j", p=P))
         offsets = keep.tile([P, S // 16], U16, name="offsets")
@@ -88,12 +87,12 @@ def tile_picked_modgate_linnone_po_kernel(
 
         dealt = [
             shared.tile([P, 2, P, PACK], BF16, name=f"dealt{u}", align_bytes=64, offset=at)
-            for u, at in enumerate((AT_EARLY, AT_LATE))
+            for u, at in enumerate((AT_EARLY, AT_EARLY))
         ]
 
-        def deal(copy, u, h):
-            src = w_raw[h][:].rearrange("p j (m t) -> p m j t", t=PACK)[:, :, :, 2 * u : 2 * u + 2]
-            dst = dealt[u][:].rearrange("p t m j -> p m j t")[:, :, 2 * h : 2 * h + 2, :]
+        def deal(copy, u, h, t0=0, t1=2):
+            src = w_raw[h][:].rearrange("p j (m t) -> p m j t", t=PACK)[:, :, :, 2 * u + t0 : 2 * u + t1]
+            dst = dealt[u][:].rearrange("p t m j -> p m j t")[:, :, 2 * h : 2 * h + 2, t0:t1]
             copy(dst, src)
 
         weights = {}
@@ -132,7 +131,8 @@ def tile_picked_modgate_linnone_po_kernel(
             return placed[t][:].indirect(offsets[:, s0 // 16 : s1 // 16])
 
         deal(nc.scalar.copy, 0, 0)
-        deal(nc.vector.tensor_copy, 0, 1)
+        for t in range(2):
+            deal(nc.vector.tensor_copy, 0, 1, t, t + 1)
         picked_scores = keep.tile([P, S], F32, name="picked_scores", align_bytes=64)
         nc.scalar.activation(picked_scores[:], scores[:].indirect(offsets[:]), COPY)
         quantise_weights(0, 1)
@@ -141,14 +141,14 @@ def tile_picked_modgate_linnone_po_kernel(
         rest = product(0, LEAD, HALF, S)
         whole = {1: product(1, 0, S)}
         deal(nc.vector.tensor_copy, 1, 0)
-        deal(nc.scalar.copy, 1, 1)
 
         out_rows = out_0.rearrange("(p t) c -> t p c", t=PACK)
         nc.scalar.activation(target(0, 0, LEAD), weigh(0, 0, LEAD, lead[:])[:], COPY)
+        deal(nc.vector.tensor_copy, 1, 1)
+        nc.scalar.activation(target(0, LEAD, S), weigh(0, LEAD, S, rest[:])[:], COPY)
         quantise_weights(2, 2)
         for t in (3, 2):
             whole[t] = product(t, 0, S)
-        nc.scalar.activation(target(0, LEAD, S), weigh(0, LEAD, S, rest[:])[:], COPY)
         nc.sync.dma_start(out_rows[0], placed[0][:])
         result = {t: weigh(t, 0, S, whole[t][:]) for t in (1, 3, 2)}
         nc.scalar.activation(target(3, 0, SHARE), result[3][:, :SHARE], COPY)
@@ -173,12 +173,12 @@ def tile_picked_modgate_linnone_po_kernel(
         rounded = {}
         for c0, c1 in pieces:
             rounded[c0] = keep.tile([P, PACK * (c1 - c0)], BF16, name=f"rounded{c0}", align_bytes=64)
-            copy, word = (nc.vector.tensor_copy, I32) if c1 == T else (nc.scalar.copy, U32)
+            copy, word = (nc.vector.tensor_copy, I32) if c1 == CUTS[-2] else (nc.scalar.copy, U32)
             copy(
                 rounded[c0][:].bitcast(word).rearrange("p (c u) -> p c u", u=2),
                 paired[:, :, c0:c1].rearrange("p u c e -> p u (c e)").bitcast(word).rearrange("p u c -> p c u"),
             )
-        for group in (pieces[:2], pieces[2:3], pieces[4:], pieces[3:4]):
+        for group in (pieces[:2], pieces[2:4], pieces[4:]):
             first, last = min(group)[0], max(group)[1]
             out_codes = keep.tile([P, last - first], I32, name=f"out_codes{first}", align_bytes=64)
             for c0, c1 in group:

@@ -20,7 +20,7 @@ P = 128
 PACK = 4
 LEAD = 128
 HALF = S // 2
-SHARE = 256
+SHARE = 224
 CUTS = (0, 128, 384, 640, 896, T)
 AT_WINDOWS = 0
 AT_RAW = AT_WINDOWS + PACK * 4 * T
@@ -141,10 +141,10 @@ def tile_picked_modgate_linnone_po_kernel(
         rest = product(0, LEAD, HALF, S)
         whole = {1: product(1, 0, S)}
         deal(nc.vector.tensor_copy, 1, 0)
+        deal(nc.scalar.copy, 1, 1)
 
         out_rows = out_0.rearrange("(p t) c -> t p c", t=PACK)
         nc.scalar.activation(target(0, 0, LEAD), weigh(0, 0, LEAD, lead[:])[:], COPY)
-        deal(nc.vector.tensor_copy, 1, 1)
         nc.scalar.activation(target(0, LEAD, S), weigh(0, LEAD, S, rest[:])[:], COPY)
         quantise_weights(2, 2)
         for t in (3, 2):

@@ -20,12 +20,13 @@ P = 128
 PACK = 4
 LEAD = 128
 HALF = S // 2
-SHARE = 224
-CUTS = (0, 128, 384, 640, 896, T)
+SHARE = 192
+CUTS = (0, 256, 512, 768, T)
 AT_WINDOWS = 0
 AT_RAW = AT_WINDOWS + PACK * 4 * T
 AT_PICKED = AT_RAW + 4 * PACK * N
 AT_EARLY = AT_PICKED + 5 * S
+AT_LATE_CODES = AT_EARLY + 4 * N
 
 
 def tile_picked_modgate_linnone_po_kernel(
@@ -122,8 +123,9 @@ def tile_picked_modgate_linnone_po_kernel(
                 )
             return acc
 
-        def weigh(t, s0, s1, sums):
-            result = keep.tile([P, s1 - s0], F32, name=f"result{t}_{s0}", align_bytes=64)
+        def weigh(t, s0, s1, sums, **place):
+            pool = shared if place else keep
+            result = pool.tile([P, s1 - s0], F32, name=f"result{t}_{s0}", align_bytes=64, **place)
             nc.vector.tensor_tensor(result[:], sums, picked_scores[:, s0:s1], MULT)
             return result
 
@@ -139,22 +141,28 @@ def tile_picked_modgate_linnone_po_kernel(
         quantise_weights(1, 1)
         lead = product(0, 0, LEAD)
         rest = product(0, LEAD, HALF, S)
-        whole = {1: product(1, 0, S)}
+        lead1 = product(1, 0, LEAD)
+        rest1 = product(1, LEAD, HALF, S)
+        whole = {}
         deal(nc.vector.tensor_copy, 1, 0)
         deal(nc.scalar.copy, 1, 1)
 
         out_rows = out_0.rearrange("(p t) c -> t p c", t=PACK)
         nc.scalar.activation(target(0, 0, LEAD), weigh(0, 0, LEAD, lead[:])[:], COPY)
         nc.scalar.activation(target(0, LEAD, S), weigh(0, LEAD, S, rest[:])[:], COPY)
-        quantise_weights(2, 2)
+        lead_result1 = weigh(1, 0, LEAD, lead1[:])
+        quantise_weights(2, 2, offset=AT_LATE_CODES)
         for t in (3, 2):
             whole[t] = product(t, 0, S)
         nc.sync.dma_start(out_rows[0], placed[0][:])
-        result = {t: weigh(t, 0, S, whole[t][:]) for t in (1, 3, 2)}
+        nc.vector.tensor_copy(target(1, 0, LEAD), lead_result1[:])
+        result = {3: weigh(3, 0, S, whole[3][:])}
+        result[1] = weigh(1, LEAD, S, rest1[:], offset=AT_LATE_CODES)
+        result[2] = weigh(2, 0, S, whole[2][:])
         nc.scalar.activation(target(3, 0, SHARE), result[3][:, :SHARE], COPY)
         for s0, s1 in ((0, S - LEAD), (S - LEAD, S)):
             nc.scalar.activation(target(2, s0, s1), result[2][:, s0:s1], COPY)
-        nc.vector.tensor_copy(target(1, 0, S), result[1][:])
+        nc.vector.tensor_copy(target(1, LEAD, S), result[1][:])
         nc.sync.dma_start(out_rows[1], placed[1][:])
         nc.vector.tensor_copy(target(3, SHARE, S), result[3][:, SHARE:])
         nc.sync.dma_start(out_rows[3], placed[3][:])
@@ -173,12 +181,12 @@ def tile_picked_modgate_linnone_po_kernel(
         rounded = {}
         for c0, c1 in pieces:
             rounded[c0] = keep.tile([P, PACK * (c1 - c0)], BF16, name=f"rounded{c0}", align_bytes=64)
-            copy, word = (nc.vector.tensor_copy, I32) if c1 == CUTS[-2] else (nc.scalar.copy, U32)
+            copy, word = (nc.vector.tensor_copy, I32) if c1 == T else (nc.scalar.copy, U32)
             copy(
                 rounded[c0][:].bitcast(word).rearrange("p (c u) -> p c u", u=2),
                 paired[:, :, c0:c1].rearrange("p u c e -> p u (c e)").bitcast(word).rearrange("p u c -> p c u"),
             )
-        for group in (pieces[:2], pieces[2:4], pieces[4:]):
+        for group in (pieces[:1], pieces[1:2], pieces[3:], pieces[2:3]):
             first, last = min(group)[0], max(group)[1]
             out_codes = keep.tile([P, last - first], I32, name=f"out_codes{first}", align_bytes=64)
             for c0, c1 in group:

@@ -21,7 +21,7 @@ PACK = 4
 LEAD = 128
 HALF = S // 2
 SHARE = 192
-CUTS = (0, 256, 512, 768, T)
+CUTS = (0, 256, 512, 640, T)
 AT_WINDOWS = 0
 AT_RAW = AT_WINDOWS + PACK * 4 * T
 AT_PICKED = AT_RAW + 4 * PACK * N
@@ -173,7 +173,7 @@ def tile_picked_modgate_linnone_po_kernel(
             nc.gpsimd.tensor_scalar(paired[:, 0, :, t], placed[t][:], 1.0, 0.0, MULT, ADD)
         nc.vector.tensor_copy(paired[:, 1, :, 1], placed[3][:])
         pieces = list(zip(CUTS, CUTS[1:]))
-        for c0, c1 in pieces:
+        for c0, c1 in pieces[:1] + pieces[-1:] + pieces[1:-1]:
             nc.vector.tensor_copy(paired[:, 1, c0:c1, 0], placed[2][:, c0:c1])
 
         out_scales = keep.tile([P, T], U8, name="out_scales", align_bytes=64)
@@ -186,7 +186,7 @@ def tile_picked_modgate_linnone_po_kernel(
                 rounded[c0][:].bitcast(word).rearrange("p (c u) -> p c u", u=2),
                 paired[:, :, c0:c1].rearrange("p u c e -> p u (c e)").bitcast(word).rearrange("p u c -> p c u"),
             )
-        for group in (pieces[:1], pieces[1:2], pieces[3:], pieces[2:3]):
+        for group in (pieces[:1], pieces[3:], pieces[1:2], pieces[2:3]):
             first, last = min(group)[0], max(group)[1]
             out_codes = keep.tile([P, last - first], I32, name=f"out_codes{first}", align_bytes=64)
             for c0, c1 in group:

@@ -42,11 +42,11 @@ def tile_picked_modgate_linnone_po_kernel(
         nc.vector.memset(token_scales[:].bitcast(I32), 0)
         score_home = shared.tile([P, N], F32, name="score_cols", align_bytes=64, offset=AT_EARLY)
         score_cols = score_home[:, : T // P]
-        nc.sync.dma_start(score_cols, gate[0].rearrange("(p j) -> p j", p=P))
-        offsets = keep.tile([P, S // 16], U16, name="offsets")
-        nc.sync.dma_start(offsets[:], offs)
+        nc.scalar.dma_start(score_cols, gate[0].rearrange("(p j) -> p j", p=P))
         token_words = keep.tile([P, T], I32, name="token_words", align_bytes=64)
         nc.sync.dma_start(token_words[:], x_words[0].rearrange("p c r -> p (c r)").bitcast(I32))
+        offsets = keep.tile([P, S // 16], U16, name="offsets")
+        nc.sync.dma_start(offsets[:], offs)
         for r in range(4):
             nc.sync.dma_start(token_scales[r:P:32, :].bitcast(I32), x_scales[0, r:16:4, :].bitcast(I32))
 

@@ -42,7 +42,7 @@ def tile_picked_modgate_linnone_po_kernel(
         nc.vector.memset(token_scales[:].bitcast(I32), 0)
         score_home = shared.tile([P, N], F32, name="score_cols", align_bytes=64, offset=AT_EARLY)
         score_cols = score_home[:, : T // P]
-        nc.scalar.dma_start(score_cols, gate[0].rearrange("(p j) -> p j", p=P))
+        nc.sync.dma_start(score_cols, gate[0].rearrange("(p j) -> p j", p=P))
         token_words = keep.tile([P, T], I32, name="token_words", align_bytes=64)
         nc.sync.dma_start(token_words[:], x_words[0].rearrange("p c r -> p (c r)").bitcast(I32))
         offsets = keep.tile([P, S // 16], U16, name="offsets")
@@ -141,8 +141,8 @@ def tile_picked_modgate_linnone_po_kernel(
         quantise_weights(1, 1)
         lead = product(0, 0, LEAD)
         rest = product(0, LEAD, HALF, S)
-        lead1 = product(1, 0, LEAD)
-        rest1 = product(1, LEAD, HALF, S)
+        lead1 = product(1, 0, HALF)
+        rest1 = product(1, HALF, S)
         whole = {}
         deal(nc.vector.tensor_copy, 1, 0)
         deal(nc.scalar.copy, 1, 1)
@@ -150,19 +150,19 @@ def tile_picked_modgate_linnone_po_kernel(
         out_rows = out_0.rearrange("(p t) c -> t p c", t=PACK)
         nc.scalar.activation(target(0, 0, LEAD), weigh(0, 0, LEAD, lead[:])[:], COPY)
         nc.scalar.activation(target(0, LEAD, S), weigh(0, LEAD, S, rest[:])[:], COPY)
-        lead_result1 = weigh(1, 0, LEAD, lead1[:])
+        lead_result1 = weigh(1, 0, HALF, lead1[:])
         quantise_weights(2, 2, offset=AT_LATE_CODES)
         for t in (3, 2):
             whole[t] = product(t, 0, S)
         nc.sync.dma_start(out_rows[0], placed[0][:])
-        nc.vector.tensor_copy(target(1, 0, LEAD), lead_result1[:])
+        nc.vector.tensor_copy(target(1, 0, HALF), lead_result1[:])
         result = {3: weigh(3, 0, S, whole[3][:])}
-        result[1] = weigh(1, LEAD, S, rest1[:], offset=AT_LATE_CODES)
+        result[1] = weigh(1, HALF, S, rest1[:], offset=AT_LATE_CODES)
         result[2] = weigh(2, 0, S, whole[2][:])
         nc.scalar.activation(target(3, 0, SHARE), result[3][:, :SHARE], COPY)
         for s0, s1 in ((0, S - LEAD), (S - LEAD, S)):
             nc.scalar.activation(target(2, s0, s1), result[2][:, s0:s1], COPY)
-        nc.vector.tensor_copy(target(1, LEAD, S), result[1][:])
+        nc.vector.tensor_copy(target(1, HALF, S), result[1][:])
         nc.sync.dma_start(out_rows[1], placed[1][:])
         nc.vector.tensor_copy(target(3, SHARE, S), result[3][:, SHARE:])
         nc.sync.dma_start(out_rows[3], placed[3][:])
@@ -173,7 +173,7 @@ def tile_picked_modgate_linnone_po_kernel(
             nc.gpsimd.tensor_scalar(paired[:, 0, :, t], placed[t][:], 1.0, 0.0, MULT, ADD)
         nc.vector.tensor_copy(paired[:, 1, :, 1], placed[3][:])
         pieces = list(zip(CUTS, CUTS[1:]))
-        for c0, c1 in pieces[:1] + pieces[-1:] + pieces[1:-1]:
+        for c0, c1 in (pieces[0], pieces[-1], (CUTS[1], CUTS[-2])):
             nc.vector.tensor_copy(paired[:, 1, c0:c1, 0], placed[2][:, c0:c1])
 
         out_scales = keep.tile([P, T], U8, name="out_scales", align_bytes=64)

@@ -58,8 +58,8 @@ def tile_picked_modgate_linnone_po_kernel(
         w_rows = w1.rearrange("(p j) c -> p j c", j=PACK)
         w_raw = []
         for h in range(2):
-            raw = shared.tile([P, 2, N], F32, name=f"w_raw{h}", align_bytes=64, offset=AT_RAW + 8 * N * h)
-            nc.sync.dma_start(raw[:], w_rows[:, 2 * h : 2 * h + 2, :])
+            raw = shared.tile([P, PACK, N // 2], F32, name=f"w_raw{h}", align_bytes=64, offset=AT_RAW + 8 * N * h)
+            nc.sync.dma_start(raw[:], w_rows[:, :, h * N // 2 : (h + 1) * N // 2])
             w_raw.append(raw)
 
         placed = {}
@@ -93,7 +93,7 @@ def tile_picked_modgate_linnone_po_kernel(
 
         def deal(copy, u, h, t0=0, t1=2):
             src = w_raw[h][:].rearrange("p j (m t) -> p m j t", t=PACK)[:, :, :, 2 * u + t0 : 2 * u + t1]
-            dst = dealt[u][:].rearrange("p t m j -> p m j t")[:, :, 2 * h : 2 * h + 2, t0:t1]
+            dst = dealt[u][:].rearrange("p t m j -> p m j t")[:, h * P // 2 : (h + 1) * P // 2, :, t0:t1]
             copy(dst, src)
 
         weights = {}

@@ -21,6 +21,7 @@ PACK = 4
 LEAD = 128
 HALF = S // 2
 SHARE = 192
+W_CUTS = (0, 320, N)
 CUTS = (0, 256, 512, 640, T)
 AT_WINDOWS = 0
 AT_RAW = AT_WINDOWS + PACK * 4 * T
@@ -58,8 +59,9 @@ def tile_picked_modgate_linnone_po_kernel(
         w_rows = w1.rearrange("(p j) c -> p j c", j=PACK)
         w_raw = []
         for h in range(2):
-            raw = shared.tile([P, PACK, N // 2], F32, name=f"w_raw{h}", align_bytes=64, offset=AT_RAW + 8 * N * h)
-            nc.sync.dma_start(raw[:], w_rows[:, :, h * N // 2 : (h + 1) * N // 2])
+            c0, c1 = W_CUTS[h : h + 2]
+            raw = shared.tile([P, PACK, c1 - c0], F32, name=f"w_raw{h}", align_bytes=64, offset=AT_RAW + 4 * PACK * c0)
+            nc.sync.dma_start(raw[:], w_rows[:, :, c0:c1])
             w_raw.append(raw)
 
         placed = {}
@@ -93,7 +95,7 @@ def tile_picked_modgate_linnone_po_kernel(
 
         def deal(copy, u, h, t0=0, t1=2):
             src = w_raw[h][:].rearrange("p j (m t) -> p m j t", t=PACK)[:, :, :, 2 * u + t0 : 2 * u + t1]
-            dst = dealt[u][:].rearrange("p t m j -> p m j t")[:, h * P // 2 : (h + 1) * P // 2, :, t0:t1]
+            dst = dealt[u][:].rearrange("p t m j -> p m j t")[:, W_CUTS[h] // PACK : W_CUTS[h + 1] // PACK, :, t0:t1]
             copy(dst, src)
 
         weights = {}

from contextlib import ExitStack

import concourse.mybir as mybir

K, T, S, N = 512, 1024, 512, 512
FLOPS = 2 * K * S * N

F32 = mybir.dt.float32
BF16 = mybir.dt.bfloat16
I32 = mybir.dt.int32
U32 = mybir.dt.uint32
U16 = mybir.dt.uint16
U8 = mybir.dt.uint8
FP8X4 = mybir.dt.float8_e4m3fn_x4
MULT = mybir.AluOpType.mult
ADD = mybir.AluOpType.add
COPY = mybir.ActivationFunctionType.Copy

P = 128
PACK = 4
LEAD = 128
HALF = S // 2
SHARE = 192
W_CUTS = (0, 320, N)
CUTS = (0, 256, 512, 640, T)
AT_WINDOWS = 0
AT_RAW = AT_WINDOWS + PACK * 4 * T
AT_PICKED = AT_RAW + 4 * PACK * N
AT_EARLY = AT_PICKED + 5 * S
AT_LATE_CODES = AT_EARLY + 4 * N


def tile_picked_modgate_linnone_po_kernel(
    tc, x_words, x_scales, gate, w1, offs, out_0, out_1, out_2
):
    nc = tc.nc
    with ExitStack() as ctx:
        keep = ctx.enter_context(tc.tile_pool(name="keep", bufs=1))
        psum = ctx.enter_context(tc.psum_pool(name="psum", bufs=1))
        shared = ctx.enter_context(tc.tile_pool(name="shared", bufs=1))

        token_scales = keep.tile([P, T], U8, name="token_scales", align_bytes=64)
        nc.vector.memset(token_scales[:].bitcast(I32), 0)
        score_home = shared.tile([P, N], F32, name="score_cols", align_bytes=64, offset=AT_EARLY)
        score_cols = score_home[:, : T // P]
        nc.sync.dma_start(score_cols, gate[0].rearrange("(p j) -> p j", p=P))
        token_words = keep.tile([P, T], I32, name="token_words", align_bytes=64)
        nc.sync.dma_start(token_words[:], x_words[0].rearrange("p c r -> p (c r)").bitcast(I32))
        offsets = keep.tile([P, S // 16], U16, name="offsets")
        nc.sync.dma_start(offsets[:], offs)
        for r in range(4):
            nc.sync.dma_start(token_scales[r:P:32, :].bitcast(I32), x_scales[0, r:16:4, :].bitcast(I32))

        identity = keep.tile([P, P], F32, name="identity", align_bytes=64)
        ramp = shared.tile([P, AT_EARLY // 4], F32, name="ramp", align_bytes=64, offset=AT_WINDOWS)
        nc.gpsimd.iota(ramp[:, :P], [[1, P]], base=0, channel_multiplier=-1, allow_small_or_imprecise_dtypes=True)
        nc.vector.tensor_scalar(identity[:], ramp[:, :P], 0.0, None, mybir.AluOpType.is_equal)

        w_rows = w1.rearrange("(p j) c -> p j c", j=PACK)
        w_raw = []
        for h in range(2):
            c0, c1 = W_CUTS[h : h + 2]
            raw = shared.tile([P, PACK, c1 - c0], F32, name=f"w_raw{h}", align_bytes=64, offset=AT_RAW + 4 * PACK * c0)
            nc.sync.dma_start(raw[:], w_rows[:, :, c0:c1])
            w_raw.append(raw)

        placed = {}
        for t in (0, 1, 3, 2):
            placed[t] = shared.tile([P, T], F32, name=f"placed{t}", align_bytes=64, offset=AT_WINDOWS + 4 * T * t)
            engine = nc.vector if t == 0 else nc.gpsimd
            engine.memset(placed[t][:].bitcast(I32), 0)

        scores = keep.tile([P, T], F32, name="scores", align_bytes=64)
        for b in range(2):
            spread = psum.tile([P, PACK, P], F32, name=f"spread{b}")
            for j in range(PACK):
                col = PACK * b + j
                nc.tensor.transpose(
                    spread[:, j, :], score_cols[:, col : col + 1].to_broadcast([P, P]), identity[:]
                )
            nc.scalar.copy(
                scores[:].rearrange("p (n j) -> p n j", j=T // P)[:, :, PACK * b : PACK * (b + 1)],
                spread[:].rearrange("p j n -> p n j"),
            )

        picked_scales = shared.tile([P, S], U8, name="picked_scales", align_bytes=64, offset=AT_PICKED)
        picked_words = shared.tile([P, S], U32, name="picked_words", align_bytes=64, offset=AT_PICKED + S)
        nc.vector.tensor_copy(picked_words[:], token_words[:].bitcast(U32).indirect(offsets[:]))
        nc.vector.tensor_copy(picked_scales[:], token_scales[:].indirect(offsets[:]))

        dealt = [
            shared.tile([P, 2, P, PACK], BF16, name=f"dealt{u}", align_bytes=64, offset=at)
            for u, at in enumerate((AT_EARLY, AT_EARLY))
        ]

        def deal(copy, u, h, t0=0, t1=2):
            src = w_raw[h][:].rearrange("p j (m t) -> p m j t", t=PACK)[:, :, :, 2 * u + t0 : 2 * u + t1]
            dst = dealt[u][:].rearrange("p t m j -> p m j t")[:, W_CUTS[h] // PACK : W_CUTS[h + 1] // PACK, :, t0:t1]
            copy(dst, src)

        weights = {}

        def quantise_weights(first, count, **place):
            pool = shared if place else keep
            codes = pool.tile([P, count * P], U32, name=f"w_codes{first}", align_bytes=64, **place)
            scales = keep.tile([P, count * P], U8, name=f"w_scales{first}", align_bytes=64)
            source = dealt[first // 2][:, first % 2 : first % 2 + count]
            nc.vector.quantize_mx(
                out=codes[:].bitcast(FP8X4), scales=scales[:], in_=source.rearrange("p t m j -> p (t m j)")
            )
            for i in range(count):
                weights[first + i] = (codes[:, i * P : (i + 1) * P], scales[:, i * P : (i + 1) * P])

        def product(t, *cuts):
            acc = psum.tile([P, cuts[-1] - cuts[0]], F32, name=f"acc{t}_{cuts[0]}")
            for s0, s1 in zip(cuts, cuts[1:]):
                nc.tensor.matmul_mx(
                    out=acc[:, s0 - cuts[0] : s1 - cuts[0]],
                    lhsT=weights[t][0].bitcast(FP8X4),
                    lhsT_scale=weights[t][1],
                    rhs=picked_words[:, s0:s1].bitcast(FP8X4),
                    rhs_scale=picked_scales[:, s0:s1],
                    start=True,
                    stop=True,
                )
            return acc

        def weigh(t, s0, s1, sums, **place):
            pool = shared if place else keep
            result = pool.tile([P, s1 - s0], F32, name=f"result{t}_{s0}", align_bytes=64, **place)
            nc.vector.tensor_tensor(result[:], sums, picked_scores[:, s0:s1], MULT)
            return result

        def target(t, s0, s1):
            return placed[t][:].indirect(offsets[:, s0 // 16 : s1 // 16])

        deal(nc.scalar.copy, 0, 0)
        for t in range(2):
            deal(nc.vector.tensor_copy, 0, 1, t, t + 1)
        picked_scores = keep.tile([P, S], F32, name="picked_scores", align_bytes=64)
        nc.scalar.activation(picked_scores[:], scores[:].indirect(offsets[:]), COPY)
        quantise_weights(0, 1)
        quantise_weights(1, 1)
        lead = product(0, 0, LEAD)
        rest = product(0, LEAD, HALF, S)
        lead1 = product(1, 0, HALF)
        rest1 = product(1, HALF, S)
        whole = {}
        deal(nc.vector.tensor_copy, 1, 0)
        deal(nc.scalar.copy, 1, 1)

        out_rows = out_0.rearrange("(p t) c -> t p c", t=PACK)
        nc.scalar.activation(target(0, 0, LEAD), weigh(0, 0, LEAD, lead[:])[:], COPY)
        nc.scalar.activation(target(0, LEAD, S), weigh(0, LEAD, S, rest[:])[:], COPY)
        lead_result1 = weigh(1, 0, HALF, lead1[:])
        quantise_weights(2, 2, offset=AT_LATE_CODES)
        for t in (3, 2):
            whole[t] = product(t, 0, S)
        nc.sync.dma_start(out_rows[0], placed[0][:])
        nc.vector.tensor_copy(target(1, 0, HALF), lead_result1[:])
        result = {3: weigh(3, 0, S, whole[3][:])}
        result[1] = weigh(1, HALF, S, rest1[:], offset=AT_LATE_CODES)
        result[2] = weigh(2, 0, S, whole[2][:])
        nc.scalar.activation(target(3, 0, SHARE), result[3][:, :SHARE], COPY)
        for s0, s1 in ((0, S - LEAD), (S - LEAD, S)):
            nc.scalar.activation(target(2, s0, s1), result[2][:, s0:s1], COPY)
        nc.vector.tensor_copy(target(1, HALF, S), result[1][:])
        nc.sync.dma_start(out_rows[1], placed[1][:])
        nc.vector.tensor_copy(target(3, SHARE, S), result[3][:, SHARE:])
        nc.sync.dma_start(out_rows[3], placed[3][:])
        nc.sync.dma_start(out_rows[2], placed[2][:])

        paired = keep.tile([P, 2, T, 2], BF16, name="paired", align_bytes=64)
        for t in (0, 1):
            nc.gpsimd.tensor_scalar(paired[:, 0, :, t], placed[t][:], 1.0, 0.0, MULT, ADD)
        nc.vector.tensor_copy(paired[:, 1, :, 1], placed[3][:])
        pieces = list(zip(CUTS, CUTS[1:]))
        for c0, c1 in (pieces[0], pieces[-1], (CUTS[1], CUTS[-2])):
            nc.vector.tensor_copy(paired[:, 1, c0:c1, 0], placed[2][:, c0:c1])

        out_scales = keep.tile([P, T], U8, name="out_scales", align_bytes=64)
        words_hbm = out_1[0].rearrange("p c r -> p (c r)").bitcast(I32)
        rounded = {}
        for c0, c1 in pieces:
            rounded[c0] = keep.tile([P, PACK * (c1 - c0)], BF16, name=f"rounded{c0}", align_bytes=64)
            copy, word = (nc.vector.tensor_copy, I32) if c1 == T else (nc.scalar.copy, U32)
            copy(
                rounded[c0][:].bitcast(word).rearrange("p (c u) -> p c u", u=2),
                paired[:, :, c0:c1].rearrange("p u c e -> p u (c e)").bitcast(word).rearrange("p u c -> p c u"),
            )
        for group in (pieces[:1], pieces[3:], pieces[1:2], pieces[2:3]):
            first, last = min(group)[0], max(group)[1]
            out_codes = keep.tile([P, last - first], I32, name=f"out_codes{first}", align_bytes=64)
            for c0, c1 in group:
                nc.vector.quantize_mx(
                    out=out_codes[:, c0 - first : c1 - first].bitcast(FP8X4),
                    scales=out_scales[:, c0:c1],
                    in_=rounded[c0][:],
                )
            nc.sync.dma_start(words_hbm[:, first:last], out_codes[:])
        for r in range(4):
            queue = nc.scalar if r == 0 else nc.sync
            queue.dma_start(out_2[0, r:16:4, :].bitcast(I32), out_scales[r:P:32, :].bitcast(I32))
